import numpy as np
import ml_dtypes


def mxq(x, axis, fmt="e4m3"):
    dtype, down = {"e4m3": (ml_dtypes.float8_e4m3fn, 7), "e5m2": (ml_dtypes.float8_e5m2, 14)}[fmt]
    v = np.moveaxis(np.asarray(x, np.float32).astype(ml_dtypes.bfloat16).astype(np.float64), axis, -1)
    blocks = v.reshape(v.shape[:-1] + (-1, 32))
    amax = np.abs(blocks).max(-1, keepdims=True)
    byte = np.maximum(np.where(amax > 0, np.frexp(amax)[1] - 1 + 127, 0) - down, 1)
    scale = np.exp2(byte - 127.0)
    codes = (blocks / scale).astype(np.float32).astype(dtype).astype(np.float64)
    return np.moveaxis((codes * scale).reshape(v.shape), -1, axis)


WIDE = False


def mx_kscale(k):
    if not WIDE:
        return np.ones(k)
    levels = np.array([10, -10, 5, -5, 0])
    if k % 512:
        return np.exp2(np.random.permutation(np.resize(levels, k // 32))).repeat(32)
    a = np.empty((k // 512, 16))
    for p in range(k // 512):
        a[p, :8] = np.random.permutation(np.resize(levels, 8))
        for g in range(8):
            far = levels[np.abs(levels - a[p, g]) >= 10]
            a[p, g + 8] = far[np.random.randint(len(far))]
    return np.exp2(a.ravel()).repeat(32)


def f64(x):
    return np.asarray(x).astype(np.float64)


def striped(idx):
    return np.tile(idx.reshape(-1, 16).T, (8, 1)).astype(np.uint16)


def unstriped(offs):
    return offs[:16].T.reshape(-1).astype(np.int64)


def pack_weight(w):
    k, n = w.shape
    w = f64(np.asarray(w, np.float32).astype(ml_dtypes.bfloat16)).reshape(k // 32, 32, n)
    amax = np.abs(w).max(1)
    byte = np.clip(np.where(amax > 0, np.frexp(amax)[1] - 1 + 127 - 7, 1), 1, 254)
    scaled = (w * np.exp2(127.0 - byte)[:, None, :]).reshape(k, n).astype(np.float32)
    words = np.ascontiguousarray(scaled.reshape(k // 512, 128, 4, n).transpose(0, 1, 3, 2)).astype(ml_dtypes.float8_e4m3fn).view(np.uint8)
    return words, np.ascontiguousarray(byte.astype(np.uint8).reshape(k // 512, 16, n))


def unpack_weight(words, scales):
    g, p, n, _ = words.shape
    vals = np.ascontiguousarray(words).view(ml_dtypes.float8_e4m3fn).astype(np.float64) * np.repeat(np.exp2(scales.astype(np.float64) - 127.0), 8, axis=1)[..., None]
    return vals.transpose(0, 1, 3, 2).reshape(g * 512, n)


E2M1 = np.array([0.0, 0.5, 1.0, 1.5, 2.0, 3.0, 4.0, 6.0, -0.0, -0.5, -1.0, -1.5, -2.0, -3.0, -4.0, -6.0])


def pack_fp4(w):
    k, n = w.shape
    w = f64(np.asarray(w, np.float32).astype(ml_dtypes.bfloat16)).reshape(k // 32, 32, n)
    amax = np.abs(w).max(1)
    mant, ex = np.frexp(amax / 6.0)
    byte = np.clip(np.where(amax > 0, np.where(mant > 0.5, ex, ex - 1) + 127, 1), 1, 254)
    scaled = (w * np.exp2(127.0 - byte)[:, None, :]).reshape(k, n).astype(np.float32)
    c = np.ascontiguousarray(scaled.reshape(k // 512, 128, 4, n).transpose(0, 1, 3, 2)).astype(ml_dtypes.float4_e2m1fn).view(np.uint8) & 0xF
    words = (c[..., 0::2] | (c[..., 1::2] << 4)).reshape(k // 512, 128, 2 * n)
    return np.ascontiguousarray(words), np.ascontiguousarray(byte.astype(np.uint8).reshape(k // 512, 16, n))


def unpack_fp4(words, scales):
    g, _, n = scales.shape
    words = np.ascontiguousarray(words).reshape(g, 128, n, 2)
    nib = np.empty((g, 128, n, 4), np.uint8)
    nib[..., 0::2] = words & 0xF
    nib[..., 1::2] = words >> 4
    vals = E2M1[nib] * np.repeat(np.exp2(scales.astype(np.float64) - 127.0), 8, axis=1)[..., None]
    return vals.transpose(0, 1, 3, 2).reshape(g * 512, n)


def planes(y):
    n, m = y.shape
    v = y.astype(np.float32).astype(ml_dtypes.bfloat16).astype(np.float64).reshape(n // 32, 32, m)
    top = np.abs(v).max(1)
    byte = np.clip(np.where(top > 0, np.frexp(top)[1] - 1 + 127 - 7, 1), 1, 254)
    codes = (v * np.exp2(127.0 - byte)[:, None, :]).reshape(n, m).astype(np.float32).astype(ml_dtypes.float8_e4m3fn).view(np.uint8)
    words = codes.reshape(n // 512, 128, 4, m).transpose(0, 1, 3, 2)
    return np.ascontiguousarray(words), np.ascontiguousarray(byte.astype(np.uint8).reshape(n // 512, 16, m))


def gelu(v):
    return 0.5 * v * (1.0 + np.tanh(np.sqrt(2.0 / np.pi) * (v + 0.044715 * v**3)))


K, T, S, H, N = 1024, 4096, 1024, 512, 512
P = 2 ** 7


def setup_inputs():
    n = np.random.standard_normal
    s = mx_kscale(K)[:, None]
    u = mx_kscale(H)
    packed_xT = pack_weight(n((K, T)) * s)
    packed_w2 = pack_fp4(n((H, N)) / np.sqrt(H) / u[:, None])
    return {
        "x_words": packed_xT[0],
        "x_scales": packed_xT[1],
        "w1": (n((K, H)) / np.sqrt(K) / s * u).astype(np.float32),
        "gain": (np.tile(np.random.uniform(0.5, 1.5, T), (P, 1))).astype(np.float32),
        "shift": (np.tile(0.5 * np.random.standard_normal(T), (P, 1))).astype(np.float32),
        "wsum": (n((H, 1)) * u[:, None]).astype(np.float32),
        "w2_words": packed_w2[0],
        "w2_scales": packed_w2[1],
        "offs": striped(np.random.permutation(T)[:S]),
    }


def reference(x_words, x_scales, w1, gain, shift, wsum, w2_words, w2_scales, offs):
    xq = unpack_weight(x_words, x_scales)[:, unstriped(offs)]
    y = mxq(f64(w1), 0, "e4m3").T @ xq
    g = f64(gain)[:1][:, unstriped(offs)]
    t = f64(shift)[:1][:, unstriped(offs)]
    h = gelu(y * g + f64(wsum) * t)
    out_0 = unpack_fp4(w2_words, w2_scales).T @ mxq(h, 0, "e4m3")
    return (out_0,) + planes(out_0)

@@ -1,0 +1,279 @@
+from contextlib import ExitStack
+
+import concourse.mybir as mybir
+from concourse.masks import make_identity
+
+K, T, S, H, N = 1024, 4096, 1024, 512, 512
+FLOPS = 2 * K * H * S + 2 * H * N * S
+
+F32 = mybir.dt.float32
+BF16 = mybir.dt.bfloat16
+I32 = mybir.dt.int32
+U32 = mybir.dt.uint32
+U16 = mybir.dt.uint16
+U8 = mybir.dt.uint8
+FP8X4 = mybir.dt.float8_e4m3fn_x4
+FP4X4 = mybir.dt.float4_e2m1fn_x4
+ACT = mybir.ActivationFunctionType
+MULT = mybir.AluOpType.mult
+ADD = mybir.AluOpType.add
+
+P = 128
+PACK = 4
+TILES = S // P
+UNIT = 2 * P
+GAIN_ROW = P - 2
+
+
+def interleave_views(dst, src):
+    return (
+        dst.rearrange("p (c i) t -> p c t i", i=4),
+        src.rearrange("p t (c i) -> p c t i", i=4),
+    )
+
+
+def tile_picked_zdq_mlpgelu_po_kernel(
+    tc, x_words, x_scales, w1, gain, shift, wsum, w2_words, w2_scales, offs, out_0, out_1, out_2
+):
+    nc = tc.nc
+    with ExitStack() as ctx:
+        keep = ctx.enter_context(tc.tile_pool(name="keep", bufs=1))
+        psum = ctx.enter_context(tc.psum_pool(name="psum", bufs=1))
+
+        def sb(name, shape, dtype, tag=None):
+            return keep.tile(shape, dtype, name=name, tag=tag or name, align_bytes=64)
+
+        def bank(index, name):
+            return psum.tile([P, 512], F32, name=name, tag="bank%d" % index)
+
+        offsets = keep.tile([P, S // 16], U16, name="offsets")
+        nc.sync.dma_start(offsets[:], offs)
+        gs_window = sb("gs_window", [P, T], F32)
+        nc.sync.dma_start(gs_window[GAIN_ROW : GAIN_ROW + 1, :], gain[0:1, :])
+        nc.sync.dma_start(gs_window[GAIN_ROW + 1 : P, :], shift[0:1, :])
+        wsum_cols = sb("wsum_cols", [P, PACK], F32)
+        nc.sync.dma_start(wsum_cols[:], wsum.rearrange("(p t) o -> p (t o)", t=PACK))
+        w2_raw = sb("w2_raw", [P, 2 * N], U8)
+        nc.sync.dma_start(w2_raw[:].bitcast(I32), w2_words[0].bitcast(I32))
+
+        x_window = [sb("x_window%d" % o, [P, T], I32) for o in range(2)]
+        w1_rows = w1.rearrange("(o p t) c -> o p t c", p=P, t=PACK)
+        w1_pieces = [(0, 0, H), (1, 0, H // 2), (1, H // 2, H)]
+        w1_raw = [sb("w1_raw%d" % n, [P, PACK, b - a], F32) for n, (o, a, b) in enumerate(w1_pieces)]
+
+        def load_x(o):
+            nc.sync.dma_start(x_window[o][:], x_words[o].rearrange("p n t -> p (n t)").bitcast(I32))
+
+        def load_w1(n):
+            o, a, b = w1_pieces[n]
+            nc.sync.dma_start(w1_raw[n][:], w1_rows[o, :, :, a:b])
+
+        load_x(0)
+        load_w1(0)
+        load_x(1)
+        load_w1(1)
+        load_w1(2)
+
+        warm = sb("warm", [P, 1], F32)
+        nc.vector.memset(warm[:], 0.0)
+        nc.scalar.activation(warm[:], warm[:], ACT.Gelu_apprx_tanh)
+
+        ident = sb("ident", [P, P], F32)
+        make_identity(nc, ident[:])
+        xs_window = sb("xs_window", [P, T], U8)
+        nc.vector.memset(xs_window[:].bitcast(I32), 0)
+        w2s_raw = sb("w2s_raw", [P, N], U8)
+        nc.vector.memset(w2s_raw[:].bitcast(I32), 0)
+        nc.vector.memset(gs_window[0:GAIN_ROW, :].bitcast(I32), 0)
+        for q in range(4):
+            nc.gpsimd.dma_start(
+                xs_window[32 * q : 32 * q + 8, :].bitcast(I32), x_scales[:, 4 * q : 4 * q + 4, :].bitcast(I32)
+            )
+        for q in range(4):
+            nc.gpsimd.dma_start(
+                w2s_raw[32 * q : 32 * q + 4, :].bitcast(I32), w2_scales[0, 4 * q : 4 * q + 4, :].bitcast(I32)
+            )
+
+        wsum_bank = bank(7, "wsum_bank")
+        for t in range(PACK):
+            nc.tensor.transpose(
+                wsum_bank[:, t * P : (t + 1) * P], wsum_cols[:, t : t + 1].to_broadcast([P, P]), ident[:]
+            )
+        wsum_rows = sb("wsum_rows", [P, H], F32)
+        nc.scalar.copy(wsum_rows[:], wsum_bank[:])
+
+        gs_picked = sb("gs_picked", [P, S], F32)
+        nc.vector.tensor_copy(gs_picked[:], gs_window[:].indirect(offsets[:]))
+        gs_cols = sb("gs_cols", [P, TILES, 2], F32)
+        for half in range(2):
+            gs_bank = bank(5 + half, "gs_bank%d" % half)
+            for n in range(4):
+                j = 4 * half + n
+                nc.tensor.transpose(gs_bank[:, n * P : (n + 1) * P], gs_picked[:, j * P : (j + 1) * P], ident[:])
+            nc.scalar.copy(
+                gs_cols[:, 4 * half : 4 * half + 4, :],
+                gs_bank[:].rearrange("p (n c) -> p n c", n=4)[:, :, GAIN_ROW:P],
+            )
+
+        w2_codes = sb("w2_codes", [P, PACK, 2 * P], U8)
+        nc.vector.tensor_copy(
+            w2_codes[:].rearrange("p t (m b) -> p t m b", b=2), w2_raw[:].rearrange("p (m t b) -> p t m b", t=PACK, b=2)
+        )
+
+        x0_picked = sb("x0_picked", [P, S], U32, "gs_window")
+        nc.vector.tensor_copy(x0_picked[:], x_window[0][:].bitcast(U32).indirect(offsets[:]))
+        xs_picked = sb("xs_picked", [P, S], U8, "x_window0")
+        nc.vector.tensor_copy(xs_picked[:], xs_window[:].indirect(offsets[:]))
+
+        w1_codes = [sb("w1_codes%d" % o, [P, H], U32) for o in range(2)]
+        w1_scales = [sb("w1_scales%d" % o, [P, H], U8) for o in range(2)]
+
+        def quantize_w1(n, split, tag):
+            o, a, b = w1_pieces[n]
+            width = b - a
+            grouped = sb("w1_grouped%d" % n, [P, width, PACK], BF16, tag)
+            if split > 0:
+                dst, src = interleave_views(grouped[:, :split, :], w1_raw[n][:, :, :split])
+                nc.scalar.copy(dst, src)
+            if split < width:
+                dst, src = interleave_views(grouped[:, split:, :], w1_raw[n][:, :, split:])
+                nc.vector.tensor_copy(dst, src)
+            nc.vector.quantize_mx(
+                w1_codes[o][:, a:b].bitcast(FP8X4), w1_scales[o][:, a:b], grouped[:].rearrange("p c t -> p (c t)")
+            )
+
+        offset_term = [sb("offset_term%d" % j, [P, H], F32) for j in range(TILES)]
+
+        def make_offset_term(j):
+            nc.scalar.activation(offset_term[j][:], wsum_rows[:], ACT.Copy, scale=gs_cols[:, j, 1:2])
+
+        for j in range(2):
+            make_offset_term(j)
+        quantize_w1(0, H, "gs_picked")
+        for j in range(2, TILES - 1):
+            make_offset_term(j)
+
+        w2s = sb("w2s", [P, PACK, P], U8, "xs_window")
+        nc.vector.tensor_copy(w2s[:], w2s_raw[:].rearrange("p (m t) -> p t m", t=PACK))
+
+        y_banks = [bank(j, "y_bank%d" % j) for j in range(TILES)]
+
+        def first_layer(j, o, codes):
+            nc.tensor.matmul_mx(
+                y_banks[j][:],
+                lhsT=codes[:, j * P : (j + 1) * P].bitcast(FP8X4),
+                lhsT_scale=xs_picked[4 * o : P, j * P : (j + 1) * P],
+                rhs=w1_codes[o][:].bitcast(FP8X4),
+                rhs_scale=w1_scales[o][:],
+                start=(o == 0),
+                stop=(o == 1),
+            )
+
+        for j in range(TILES):
+            first_layer(j, 0, x0_picked)
+
+        x1_picked = sb("x1_picked", [P, S], U32, "gs_picked")
+        for half in range(2):
+            nc.vector.tensor_copy(
+                x1_picked[:, half * 512 : (half + 1) * 512],
+                x_window[1][:].bitcast(U32).indirect(offsets[:, 32 * half : 32 * half + 32]),
+            )
+        quantize_w1(1, H // 2, "w1_raw0")
+        quantize_w1(2, 96, "w1_raw1")
+        for j in range(TILES - 1, TILES):
+            make_offset_term(j)
+
+        out_scales = sb("out_scales", [P, S], U8)
+        out_rows = out_0.rearrange("(p t) j -> p t j", t=PACK)
+        out_words = out_1[0].rearrange("p j r -> p (j r)").bitcast(I32)
+
+        units = S // UNIT
+        h_grouped = [sb("h_grouped%d" % u, [P, UNIT, PACK], BF16) for u in range(units)]
+        result = [sb("result%d" % u, [P, PACK, UNIT], F32) for u in range(units)]
+        out_grouped = [sb("out_grouped%d" % u, [P, UNIT, PACK], BF16) for u in range(units)]
+
+        def hidden(j):
+            first_layer(j, 1, x1_picked)
+            pre = sb("pre%d" % j, [P, PACK, P], F32)
+            nc.vector.scalar_tensor_tensor(
+                pre[:],
+                y_banks[j][:].rearrange("p (m t) -> p t m", t=PACK),
+                gs_cols[:, j, 0:1],
+                offset_term[j][:].rearrange("p (t m) -> p t m", t=PACK),
+                MULT,
+                ADD,
+            )
+            turned = bank(j, "turned%d" % j)
+            for t in range(PACK):
+                nc.tensor.transpose(turned[:, t * P : (t + 1) * P], pre[:, t, :], ident[:])
+            nc.scalar.activation(
+                h_grouped[j // 2][:, (j % 2) * P : (j % 2 + 1) * P, :],
+                turned[:].rearrange("p (t j) -> p j t", t=PACK),
+                ACT.Gelu_apprx_tanh,
+            )
+
+        def product(out, t, codes, scales):
+            nc.tensor.matmul_mx(
+                out,
+                lhsT=w2_codes[:, t, :].bitcast(FP4X4),
+                lhsT_scale=w2s[:, t, :],
+                rhs=codes.bitcast(FP8X4),
+                rhs_scale=scales,
+                start=True,
+                stop=True,
+            )
+
+        def second_layer(u):
+            h_codes = sb("h_codes%d" % u, [P, UNIT], U32)
+            h_scales = sb("h_scales%d" % u, [P, UNIT], U8)
+            nc.vector.quantize_mx(h_codes[:].bitcast(FP8X4), h_scales[:], h_grouped[u][:].rearrange("p j t -> p (j t)"))
+            banks = [bank(2 * u + n, "out_bank%d" % (2 * u + n)) for n in range(2)]
+            if u < units - 1:
+                for n in range(2):
+                    for e in range(2):
+                        product(banks[n][:, e * UNIT : (e + 1) * UNIT], 2 * n + e, h_codes[:], h_scales[:])
+                    nc.scalar.copy(result[u][:, 2 * n : 2 * n + 2, :].rearrange("p t j -> p (t j)"), banks[n][:])
+                nc.sync.dma_start(out_rows[:, :, u * UNIT : (u + 1) * UNIT], result[u][:])
+            else:
+                for n in (1, 0):
+                    cols = slice(n * P, (n + 1) * P)
+                    for t in range(PACK):
+                        product(banks[n][:, t * P : (t + 1) * P], t, h_codes[:, cols], h_scales[:, cols])
+                nc.vector.tensor_copy(out_grouped[u][:, P:, :], banks[1][:].rearrange("p (t j) -> p j t", t=PACK))
+                for n in range(2):
+                    cols = slice(n * P, (n + 1) * P)
+                    nc.scalar.copy(result[u][:, :, cols], banks[n][:].rearrange("p (t j) -> p t j", t=PACK))
+                    nc.sync.dma_start(out_rows[:, :, u * UNIT + n * P : u * UNIT + (n + 1) * P], result[u][:, :, cols])
+
+        def planes(u):
+            width = UNIT if u < units - 1 else P
+            dst, src = interleave_views(out_grouped[u][:, :width, :], result[u][:, :, :width])
+            nc.vector.tensor_copy(dst, src)
+            cols = slice(u * UNIT, (u + 1) * UNIT)
+            out_codes = sb("out_codes%d" % u, [P, UNIT], I32)
+            nc.vector.quantize_mx(
+                out_codes[:].bitcast(FP8X4), out_scales[:, cols], out_grouped[u][:].rearrange("p j t -> p (j t)")
+            )
+            nc.scalar.dma_start(out_words[:, cols], out_codes[:]) if u == units - 1 else nc.sync.dma_start(out_words[:, cols], out_codes[:])
+
+        hidden(0)
+        hidden(1)
+        hidden(2)
+        hidden(3)
+        second_layer(0)
+        hidden(4)
+        hidden(5)
+        second_layer(1)
+        planes(0)
+        hidden(6)
+        hidden(7)
+        second_layer(2)
+        planes(1)
+        second_layer(3)
+        planes(2)
+        planes(3)
+        for q in range(4):
+            engine = nc.sync if q < 3 else nc.scalar
+            engine.dma_start(
+                out_2[0, 4 * q : 4 * q + 4, :].bitcast(I32), out_scales[32 * q : 32 * q + 4, :].bitcast(I32)
+            )

@@ -23,6 +23,7 @@ PACK = 4
 TILES = S // P
 UNIT = 2 * P
 GAIN_ROW = P - 2
+KB = 1024
 
 
 def interleave_views(dst, src):
@@ -38,60 +39,53 @@ def tile_picked_zdq_mlpgelu_po_kernel(
     nc = tc.nc
     with ExitStack() as ctx:
         keep = ctx.enter_context(tc.tile_pool(name="keep", bufs=1))
+        reuse = ctx.enter_context(tc.tile_pool(name="reuse", bufs=1))
         psum = ctx.enter_context(tc.psum_pool(name="psum", bufs=1))
 
         def sb(name, shape, dtype, tag=None):
             return keep.tile(shape, dtype, name=name, tag=tag or name, align_bytes=64)
+
+        def placed(name, shape, dtype, offset):
+            return reuse.tile(shape, dtype, name=name, align_bytes=64, offset=offset)
 
         def bank(index, name):
             return psum.tile([P, 512], F32, name=name, tag="bank%d" % index)
 
         offsets = keep.tile([P, S // 16], U16, name="offsets")
         nc.sync.dma_start(offsets[:], offs)
-        gs_window = sb("gs_window", [P, T], F32)
-        nc.sync.dma_start(gs_window[GAIN_ROW : GAIN_ROW + 1, :], gain[0:1, :])
+        gs_window = placed("gs_window", [P, T], F32, 0)
+        nc.scalar.dma_start(gs_window[GAIN_ROW : GAIN_ROW + 1, :], gain[0:1, :])
         nc.sync.dma_start(gs_window[GAIN_ROW + 1 : P, :], shift[0:1, :])
         wsum_cols = sb("wsum_cols", [P, PACK], F32)
         nc.sync.dma_start(wsum_cols[:], wsum.rearrange("(p t) o -> p (t o)", t=PACK))
-        w2_raw = sb("w2_raw", [P, 2 * N], U8)
-        nc.sync.dma_start(w2_raw[:].bitcast(I32), w2_words[0].bitcast(I32))
 
-        x_window = [sb("x_window%d" % o, [P, T], I32) for o in range(2)]
         w1_rows = w1.rearrange("(o p t) c -> o p t c", p=P, t=PACK)
         w1_pieces = [(0, 0, H), (1, 0, H // 2), (1, H // 2, H)]
-        w1_raw = [sb("w1_raw%d" % n, [P, PACK, b - a], F32) for n, (o, a, b) in enumerate(w1_pieces)]
 
-        def load_x(o):
-            nc.sync.dma_start(x_window[o][:], x_words[o].rearrange("p n t -> p (n t)").bitcast(I32))
+        def load_x(o, window):
+            nc.sync.dma_start(window[:], x_words[o].rearrange("p n t -> p (n t)").bitcast(I32))
+            return window
 
-        def load_w1(n):
+        def load_w1(n, raw):
             o, a, b = w1_pieces[n]
-            nc.sync.dma_start(w1_raw[n][:], w1_rows[o, :, :, a:b])
+            nc.sync.dma_start(raw[:], w1_rows[o, :, :, a:b])
+            return raw
 
-        load_x(0)
-        load_w1(0)
-        load_x(1)
-        load_w1(1)
-        load_w1(2)
-
-        warm = sb("warm", [P, 1], F32)
-        nc.vector.memset(warm[:], 0.0)
-        nc.scalar.activation(warm[:], warm[:], ACT.Gelu_apprx_tanh)
+        x0_window = load_x(0, sb("x0_window", [P, T], I32))
+        w2_raw = sb("w2_raw", [P, 2 * N], U8)
+        nc.sync.dma_start(w2_raw[:].bitcast(I32), w2_words[0].bitcast(I32))
 
         ident = sb("ident", [P, P], F32)
         make_identity(nc, ident[:])
         xs_window = sb("xs_window", [P, T], U8)
         nc.vector.memset(xs_window[:].bitcast(I32), 0)
-        w2s_raw = sb("w2s_raw", [P, N], U8)
-        nc.vector.memset(w2s_raw[:].bitcast(I32), 0)
+        warm = sb("warm", [P, 1], F32)
+        nc.vector.memset(warm[:], 0.0)
         nc.vector.memset(gs_window[0:GAIN_ROW, :].bitcast(I32), 0)
+        nc.scalar.activation(warm[:], warm[:], ACT.Gelu_apprx_tanh)
         for q in range(4):
-            nc.gpsimd.dma_start(
+            nc.scalar.dma_start(
                 xs_window[32 * q : 32 * q + 8, :].bitcast(I32), x_scales[:, 4 * q : 4 * q + 4, :].bitcast(I32)
-            )
-        for q in range(4):
-            nc.gpsimd.dma_start(
-                w2s_raw[32 * q : 32 * q + 4, :].bitcast(I32), w2_scales[0, 4 * q : 4 * q + 4, :].bitcast(I32)
             )
 
         wsum_bank = bank(7, "wsum_bank")
@@ -99,11 +93,21 @@ def tile_picked_zdq_mlpgelu_po_kernel(
             nc.tensor.transpose(
                 wsum_bank[:, t * P : (t + 1) * P], wsum_cols[:, t : t + 1].to_broadcast([P, P]), ident[:]
             )
+        w1_raw = [load_w1(0, placed("w1_raw0", [P, PACK, H], F32, 16 * KB))]
         wsum_rows = sb("wsum_rows", [P, H], F32)
         nc.scalar.copy(wsum_rows[:], wsum_bank[:])
 
         gs_picked = sb("gs_picked", [P, S], F32)
         nc.vector.tensor_copy(gs_picked[:], gs_window[:].indirect(offsets[:]))
+        x1_window = load_x(1, sb("x1_window", [P, T], I32))
+        w1_raw.append(load_w1(1, placed("w1_raw1", [P, PACK, H // 2], F32, 26 * KB)))
+        w1_raw.append(load_w1(2, placed("w1_raw2", [P, PACK, H // 2], F32, 32 * KB)))
+        w2s_raw = sb("w2s_raw", [P, N], U8)
+        nc.vector.memset(w2s_raw[:].bitcast(I32), 0)
+        for q in range(4):
+            nc.sync.dma_start(
+                w2s_raw[32 * q : 32 * q + 4, :].bitcast(I32), w2_scales[0, 4 * q : 4 * q + 4, :].bitcast(I32)
+            )
         gs_cols = sb("gs_cols", [P, TILES, 2], F32)
         for half in range(2):
             gs_bank = bank(5 + half, "gs_bank%d" % half)
@@ -115,85 +119,86 @@ def tile_picked_zdq_mlpgelu_po_kernel(
                 gs_bank[:].rearrange("p (n c) -> p n c", n=4)[:, :, GAIN_ROW:P],
             )
 
-        w2_codes = sb("w2_codes", [P, PACK, 2 * P], U8)
+        xs_picked = placed("xs_picked", [P, S], U8, 4 * KB)
+        nc.vector.tensor_copy(xs_picked[:], xs_window[:].indirect(offsets[:]))
+        x0_picked = placed("x0_picked", [P, S], U32, 0)
+        nc.vector.tensor_copy(x0_picked[:], x0_window[:].bitcast(U32).indirect(offsets[:]))
+        w2_codes = sb("w2_codes", [P, PACK, 2 * P], U8, "x0_window")
         nc.vector.tensor_copy(
             w2_codes[:].rearrange("p t (m b) -> p t m b", b=2), w2_raw[:].rearrange("p (m t b) -> p t m b", t=PACK, b=2)
         )
 
-        x0_picked = sb("x0_picked", [P, S], U32, "gs_window")
-        nc.vector.tensor_copy(x0_picked[:], x_window[0][:].bitcast(U32).indirect(offsets[:]))
-        xs_picked = sb("xs_picked", [P, S], U8, "x_window0")
-        nc.vector.tensor_copy(xs_picked[:], xs_window[:].indirect(offsets[:]))
-
         w1_codes = [sb("w1_codes%d" % o, [P, H], U32) for o in range(2)]
         w1_scales = [sb("w1_scales%d" % o, [P, H], U8) for o in range(2)]
 
-        def quantize_w1(n, split, tag):
+        def quantize_w1(n, split, grouped):
             o, a, b = w1_pieces[n]
-            width = b - a
-            grouped = sb("w1_grouped%d" % n, [P, width, PACK], BF16, tag)
             if split > 0:
                 dst, src = interleave_views(grouped[:, :split, :], w1_raw[n][:, :, :split])
                 nc.scalar.copy(dst, src)
-            if split < width:
+            if split < b - a:
                 dst, src = interleave_views(grouped[:, split:, :], w1_raw[n][:, :, split:])
                 nc.vector.tensor_copy(dst, src)
             nc.vector.quantize_mx(
                 w1_codes[o][:, a:b].bitcast(FP8X4), w1_scales[o][:, a:b], grouped[:].rearrange("p c t -> p (c t)")
             )
 
-        offset_term = [sb("offset_term%d" % j, [P, H], F32) for j in range(TILES)]
+        term_at = {0: 38 * KB, 1: 40 * KB, 2: 15 * KB, 3: 17 * KB, 4: 19 * KB, 5: 21 * KB, 6: 32 * KB + 512, 7: 34 * KB + 512}
+        offset_term = {}
 
         def make_offset_term(j):
+            offset_term[j] = placed("offset_term%d" % j, [P, H], F32, term_at[j])
             nc.scalar.activation(offset_term[j][:], wsum_rows[:], ACT.Copy, scale=gs_cols[:, j, 1:2])
 
         for j in range(2):
             make_offset_term(j)
-        quantize_w1(0, H, "gs_picked")
-        for j in range(2, TILES - 1):
+        quantize_w1(0, H, sb("w1_grouped0", [P, H, PACK], BF16, "gs_picked"))
+        for j in range(2, TILES - 2):
             make_offset_term(j)
-
-        w2s = sb("w2s", [P, PACK, P], U8, "xs_window")
-        nc.vector.tensor_copy(w2s[:], w2s_raw[:].rearrange("p (m t) -> p t m", t=PACK))
 
         y_banks = [bank(j, "y_bank%d" % j) for j in range(TILES)]
 
-        def first_layer(j, o, codes):
+        def first_layer(j, n, codes):
+            o, a, b = n
             nc.tensor.matmul_mx(
-                y_banks[j][:],
+                y_banks[j][:, a:b],
                 lhsT=codes[:, j * P : (j + 1) * P].bitcast(FP8X4),
                 lhsT_scale=xs_picked[4 * o : P, j * P : (j + 1) * P],
-                rhs=w1_codes[o][:].bitcast(FP8X4),
-                rhs_scale=w1_scales[o][:],
+                rhs=w1_codes[o][:, a:b].bitcast(FP8X4),
+                rhs_scale=w1_scales[o][:, a:b],
                 start=(o == 0),
-                stop=(o == 1),
+                stop=(b == H and o == 1),
             )
 
         for j in range(TILES):
-            first_layer(j, 0, x0_picked)
+            first_layer(j, (0, 0, H), x0_picked)
 
         x1_picked = sb("x1_picked", [P, S], U32, "gs_picked")
         for half in range(2):
             nc.vector.tensor_copy(
                 x1_picked[:, half * 512 : (half + 1) * 512],
-                x_window[1][:].bitcast(U32).indirect(offsets[:, 32 * half : 32 * half + 32]),
+                x1_window[:].bitcast(U32).indirect(offsets[:, 32 * half : 32 * half + 32]),
             )
-        quantize_w1(1, H // 2, "w1_raw0")
-        quantize_w1(2, 96, "w1_raw1")
-        for j in range(TILES - 1, TILES):
+        quantize_w1(1, H // 2, placed("w1_grouped1", [P, H // 2, PACK], BF16, 23 * KB))
+        quantize_w1(2, 96, placed("w1_grouped2", [P, H // 2, PACK], BF16, 26 * KB))
+        w2s = placed("w2s", [P, PACK, P], U8, 32 * KB)
+        nc.vector.tensor_copy(w2s[:], w2s_raw[:].rearrange("p (m t) -> p t m", t=PACK))
+        for j in range(TILES - 2, TILES):
             make_offset_term(j)
+
+        for j in range(TILES):
+            first_layer(j, w1_pieces[1], x1_picked)
+            first_layer(j, w1_pieces[2], x1_picked)
 
         out_scales = sb("out_scales", [P, S], U8)
         out_rows = out_0.rearrange("(p t) j -> p t j", t=PACK)
         out_words = out_1[0].rearrange("p j r -> p (j r)").bitcast(I32)
-
         units = S // UNIT
         h_grouped = [sb("h_grouped%d" % u, [P, UNIT, PACK], BF16) for u in range(units)]
+        out_banks = {}
         result = [sb("result%d" % u, [P, PACK, UNIT], F32) for u in range(units)]
-        out_grouped = [sb("out_grouped%d" % u, [P, UNIT, PACK], BF16) for u in range(units)]
 
         def hidden(j):
-            first_layer(j, 1, x1_picked)
             pre = sb("pre%d" % j, [P, PACK, P], F32)
             nc.vector.scalar_tensor_tensor(
                 pre[:],
@@ -212,64 +217,57 @@ def tile_picked_zdq_mlpgelu_po_kernel(
                 ACT.Gelu_apprx_tanh,
             )
 
-        def product(out, t, codes, scales):
-            nc.tensor.matmul_mx(
-                out,
-                lhsT=w2_codes[:, t, :].bitcast(FP4X4),
-                lhsT_scale=w2s[:, t, :],
-                rhs=codes.bitcast(FP8X4),
-                rhs_scale=scales,
-                start=True,
-                stop=True,
-            )
-
         def second_layer(u):
             h_codes = sb("h_codes%d" % u, [P, UNIT], U32)
             h_scales = sb("h_scales%d" % u, [P, UNIT], U8)
             nc.vector.quantize_mx(h_codes[:].bitcast(FP8X4), h_scales[:], h_grouped[u][:].rearrange("p j t -> p (j t)"))
-            banks = [bank(2 * u + n, "out_bank%d" % (2 * u + n)) for n in range(2)]
-            if u < units - 1:
-                for n in range(2):
-                    for e in range(2):
-                        product(banks[n][:, e * UNIT : (e + 1) * UNIT], 2 * n + e, h_codes[:], h_scales[:])
-                    nc.scalar.copy(result[u][:, 2 * n : 2 * n + 2, :].rearrange("p t j -> p (t j)"), banks[n][:])
-                nc.sync.dma_start(out_rows[:, :, u * UNIT : (u + 1) * UNIT], result[u][:])
-            else:
-                for n in (1, 0):
-                    cols = slice(n * P, (n + 1) * P)
-                    for t in range(PACK):
-                        product(banks[n][:, t * P : (t + 1) * P], t, h_codes[:, cols], h_scales[:, cols])
-                nc.vector.tensor_copy(out_grouped[u][:, P:, :], banks[1][:].rearrange("p (t j) -> p j t", t=PACK))
-                for n in range(2):
-                    cols = slice(n * P, (n + 1) * P)
-                    nc.scalar.copy(result[u][:, :, cols], banks[n][:].rearrange("p (t j) -> p t j", t=PACK))
-                    nc.sync.dma_start(out_rows[:, :, u * UNIT + n * P : u * UNIT + (n + 1) * P], result[u][:, :, cols])
+            out_banks[u] = [bank(2 * u + n, "out_bank%d" % (2 * u + n)) for n in range(2)]
+            for t in range(PACK):
+                nc.tensor.matmul_mx(
+                    out_banks[u][t // 2][:, (t % 2) * UNIT : (t % 2 + 1) * UNIT],
+                    lhsT=w2_codes[:, t, :].bitcast(FP4X4),
+                    lhsT_scale=w2s[:, t, :],
+                    rhs=h_codes[:].bitcast(FP8X4),
+                    rhs_scale=h_scales[:],
+                    start=True,
+                    stop=True,
+                )
+
+        def leave(u, copies):
+            for n in range(2):
+                copies[n](result[u][:, 2 * n : 2 * n + 2, :].rearrange("p t j -> p (t j)"), out_banks[u][n][:])
+            nc.sync.dma_start(out_rows[:, :, u * UNIT : (u + 1) * UNIT], result[u][:])
 
         def planes(u):
-            width = UNIT if u < units - 1 else P
-            dst, src = interleave_views(out_grouped[u][:, :width, :], result[u][:, :, :width])
+            out_grouped = sb("out_grouped%d" % u, [P, UNIT, PACK], BF16)
+            dst, src = interleave_views(out_grouped[:], result[u][:])
             nc.vector.tensor_copy(dst, src)
             cols = slice(u * UNIT, (u + 1) * UNIT)
             out_codes = sb("out_codes%d" % u, [P, UNIT], I32)
             nc.vector.quantize_mx(
-                out_codes[:].bitcast(FP8X4), out_scales[:, cols], out_grouped[u][:].rearrange("p j t -> p (j t)")
+                out_codes[:].bitcast(FP8X4), out_scales[:, cols], out_grouped[:].rearrange("p j t -> p (j t)")
             )
-            nc.scalar.dma_start(out_words[:, cols], out_codes[:]) if u == units - 1 else nc.sync.dma_start(out_words[:, cols], out_codes[:])
+            queue = nc.scalar if u == units - 1 else nc.sync
+            queue.dma_start(out_words[:, cols], out_codes[:])
 
         hidden(0)
         hidden(1)
         hidden(2)
         hidden(3)
-        second_layer(0)
         hidden(4)
+        second_layer(0)
         hidden(5)
-        second_layer(1)
-        planes(0)
         hidden(6)
         hidden(7)
+        second_layer(1)
+        leave(0, (nc.vector.tensor_copy, nc.vector.tensor_copy))
         second_layer(2)
-        planes(1)
         second_layer(3)
+        leave(1, (nc.scalar.copy, nc.scalar.copy))
+        leave(2, (nc.scalar.copy, nc.scalar.copy))
+        leave(3, (nc.scalar.copy, nc.scalar.copy))
+        planes(0)
+        planes(1)
         planes(2)
         planes(3)
         for q in range(4):

@@ -58,6 +58,8 @@ def tile_picked_zdq_mlpgelu_po_kernel(
         nc.sync.dma_start(gs_window[GAIN_ROW + 1 : P, :], shift[0:1, :])
         wsum_cols = sb("wsum_cols", [P, PACK], F32)
         nc.sync.dma_start(wsum_cols[:], wsum.rearrange("(p t) o -> p (t o)", t=PACK))
+        w2_raw = sb("w2_raw", [P, 2 * N], U8)
+        nc.sync.dma_start(w2_raw[:].bitcast(I32), w2_words[0].bitcast(I32))
 
         w1_rows = w1.rearrange("(o p t) c -> o p t c", p=P, t=PACK)
         w1_pieces = [(0, 0, H), (1, 0, H // 2), (1, H // 2, H)]
@@ -72,22 +74,20 @@ def tile_picked_zdq_mlpgelu_po_kernel(
             return raw
 
         x0_window = load_x(0, sb("x0_window", [P, T], I32))
-        w2_raw = sb("w2_raw", [P, 2 * N], U8)
-        nc.sync.dma_start(w2_raw[:].bitcast(I32), w2_words[0].bitcast(I32))
 
-        ident = sb("ident", [P, P], F32)
-        make_identity(nc, ident[:])
         xs_window = sb("xs_window", [P, T], U8)
-        nc.vector.memset(xs_window[:].bitcast(I32), 0)
-        warm = sb("warm", [P, 1], F32)
-        nc.vector.memset(warm[:], 0.0)
-        nc.vector.memset(gs_window[0:GAIN_ROW, :].bitcast(I32), 0)
-        nc.scalar.activation(warm[:], warm[:], ACT.Gelu_apprx_tanh)
+        nc.gpsimd.memset(xs_window[:].bitcast(I32), 0)
         for q in range(4):
-            nc.scalar.dma_start(
+            nc.gpsimd.dma_start(
                 xs_window[32 * q : 32 * q + 8, :].bitcast(I32), x_scales[:, 4 * q : 4 * q + 4, :].bitcast(I32)
             )
-
+        ident = sb("ident", [P, P], F32)
+        make_identity(nc, ident[:])
+        warm = sb("warm", [P, 1], F32)
+        nc.vector.memset(warm[:], 0.0)
+        nc.vector.memset(gs_window[0:GAIN_ROW, : T - 1].bitcast(I32), 0)
+        nc.vector.memset(gs_window[0:GAIN_ROW, T - 1 :].bitcast(I32), 0)
+        nc.scalar.activation(warm[:], warm[:], ACT.Gelu_apprx_tanh)
         wsum_bank = bank(7, "wsum_bank")
         for t in range(PACK):
             nc.tensor.transpose(
@@ -99,6 +99,10 @@ def tile_picked_zdq_mlpgelu_po_kernel(
 
         gs_picked = sb("gs_picked", [P, S], F32)
         nc.vector.tensor_copy(gs_picked[:], gs_window[:].indirect(offsets[:]))
+        w2_codes = sb("w2_codes", [P, PACK, 2 * P], U8)
+        nc.vector.tensor_copy(
+            w2_codes[:].rearrange("p t (m b) -> p t m b", b=2), w2_raw[:].rearrange("p (m t b) -> p t m b", t=PACK, b=2)
+        )
         x1_window = load_x(1, sb("x1_window", [P, T], I32))
         w1_raw.append(load_w1(1, placed("w1_raw1", [P, PACK, H // 2], F32, 26 * KB)))
         w1_raw.append(load_w1(2, placed("w1_raw2", [P, PACK, H // 2], F32, 32 * KB)))
@@ -123,10 +127,6 @@ def tile_picked_zdq_mlpgelu_po_kernel(
         nc.vector.tensor_copy(xs_picked[:], xs_window[:].indirect(offsets[:]))
         x0_picked = placed("x0_picked", [P, S], U32, 0)
         nc.vector.tensor_copy(x0_picked[:], x0_window[:].bitcast(U32).indirect(offsets[:]))
-        w2_codes = sb("w2_codes", [P, PACK, 2 * P], U8, "x0_window")
-        nc.vector.tensor_copy(
-            w2_codes[:].rearrange("p t (m b) -> p t m b", b=2), w2_raw[:].rearrange("p (m t b) -> p t m b", t=PACK, b=2)
-        )
 
         w1_codes = [sb("w1_codes%d" % o, [P, H], U32) for o in range(2)]
         w1_scales = [sb("w1_scales%d" % o, [P, H], U8) for o in range(2)]
@@ -186,10 +186,11 @@ def tile_picked_zdq_mlpgelu_po_kernel(
         for j in range(TILES - 2, TILES):
             make_offset_term(j)
 
-        for j in range(TILES):
+        for j in range(8):
             first_layer(j, w1_pieces[1], x1_picked)
             first_layer(j, w1_pieces[2], x1_picked)
 
+        out_codes = sb("out_codes", [P, S], I32)
         out_scales = sb("out_scales", [P, S], U8)
         out_rows = out_0.rearrange("(p t) j -> p t j", t=PACK)
         out_words = out_1[0].rearrange("p j r -> p (j r)").bitcast(I32)
@@ -199,18 +200,22 @@ def tile_picked_zdq_mlpgelu_po_kernel(
         result = [sb("result%d" % u, [P, PACK, UNIT], F32) for u in range(units)]
 
         def hidden(j):
+            if j >= 8:
+                first_layer(j, (1, 0, H), x1_picked)
             pre = sb("pre%d" % j, [P, PACK, P], F32)
-            nc.vector.scalar_tensor_tensor(
-                pre[:],
-                y_banks[j][:].rearrange("p (m t) -> p t m", t=PACK),
-                gs_cols[:, j, 0:1],
-                offset_term[j][:].rearrange("p (t m) -> p t m", t=PACK),
-                MULT,
-                ADD,
-            )
+            y_dealt = y_banks[j][:].rearrange("p (m t) -> p t m", t=PACK)
+            term = offset_term[j][:].rearrange("p (t m) -> p t m", t=PACK)
+            added_in_psum = j in ()
+            if added_in_psum:
+                nc.scalar.activation(pre[:], y_dealt, ACT.Copy, scale=gs_cols[:, j, 0:1])
+            else:
+                nc.vector.scalar_tensor_tensor(pre[:], y_dealt, gs_cols[:, j, 0:1], term, MULT, ADD)
             turned = bank(j, "turned%d" % j)
             for t in range(PACK):
-                nc.tensor.transpose(turned[:, t * P : (t + 1) * P], pre[:, t, :], ident[:])
+                out = turned[:, t * P : (t + 1) * P]
+                nc.tensor.matmul(out, pre[:, t, :], ident[:], start=True, stop=not added_in_psum, is_transpose=True)
+                if added_in_psum:
+                    nc.tensor.matmul(out, term[:, t, :], ident[:], start=False, stop=True, is_transpose=True)
             nc.scalar.activation(
                 h_grouped[j // 2][:, (j % 2) * P : (j % 2 + 1) * P, :],
                 turned[:].rearrange("p (t j) -> p j t", t=PACK),
@@ -236,40 +241,43 @@ def tile_picked_zdq_mlpgelu_po_kernel(
         def leave(u, copies):
             for n in range(2):
                 copies[n](result[u][:, 2 * n : 2 * n + 2, :].rearrange("p t j -> p (t j)"), out_banks[u][n][:])
-            nc.sync.dma_start(out_rows[:, :, u * UNIT : (u + 1) * UNIT], result[u][:])
+                nc.sync.dma_start(
+                    out_rows[:, 2 * n : 2 * n + 2, u * UNIT : (u + 1) * UNIT], result[u][:, 2 * n : 2 * n + 2, :]
+                )
 
-        def planes(u):
+        def planes(u, copy):
             out_grouped = sb("out_grouped%d" % u, [P, UNIT, PACK], BF16)
             dst, src = interleave_views(out_grouped[:], result[u][:])
-            nc.vector.tensor_copy(dst, src)
+            copy(dst, src)
             cols = slice(u * UNIT, (u + 1) * UNIT)
-            out_codes = sb("out_codes%d" % u, [P, UNIT], I32)
             nc.vector.quantize_mx(
-                out_codes[:].bitcast(FP8X4), out_scales[:, cols], out_grouped[:].rearrange("p j t -> p (j t)")
+                out_codes[:, cols].bitcast(FP8X4), out_scales[:, cols], out_grouped[:].rearrange("p j t -> p (j t)")
             )
-            queue = nc.scalar if u == units - 1 else nc.sync
-            queue.dma_start(out_words[:, cols], out_codes[:])
+            if u == units - 2:
+                nc.sync.dma_start(out_words[:, : S - UNIT], out_codes[:, : S - UNIT])
+            if u == units - 1:
+                nc.scalar.dma_start(out_words[:, cols], out_codes[:, cols])
 
         hidden(0)
         hidden(1)
         hidden(2)
         hidden(3)
         hidden(4)
-        second_layer(0)
         hidden(5)
+        second_layer(0)
+        leave(0, (nc.scalar.copy, nc.scalar.copy))
         hidden(6)
-        hidden(7)
         second_layer(1)
-        leave(0, (nc.vector.tensor_copy, nc.vector.tensor_copy))
-        second_layer(2)
+        leave(1, (nc.vector.tensor_copy, nc.vector.tensor_copy))
+        hidden(7)
         second_layer(3)
-        leave(1, (nc.scalar.copy, nc.scalar.copy))
+        second_layer(2)
+        planes(0, nc.vector.tensor_copy)
         leave(2, (nc.scalar.copy, nc.scalar.copy))
         leave(3, (nc.scalar.copy, nc.scalar.copy))
-        planes(0)
-        planes(1)
-        planes(2)
-        planes(3)
+        planes(1, nc.vector.tensor_copy)
+        planes(2, nc.vector.tensor_copy)
+        planes(3, nc.vector.tensor_copy)
         for q in range(4):
             engine = nc.sync if q < 3 else nc.scalar
             engine.dma_start(

@@ -75,19 +75,20 @@ def tile_picked_zdq_mlpgelu_po_kernel(
 
         x0_window = load_x(0, sb("x0_window", [P, T], I32))
 
-        xs_window = sb("xs_window", [P, T], U8)
-        nc.gpsimd.memset(xs_window[:].bitcast(I32), 0)
-        for q in range(4):
-            nc.gpsimd.dma_start(
-                xs_window[32 * q : 32 * q + 8, :].bitcast(I32), x_scales[:, 4 * q : 4 * q + 4, :].bitcast(I32)
-            )
         ident = sb("ident", [P, P], F32)
         make_identity(nc, ident[:])
+        xs_window = sb("xs_window", [P, T], U8)
+        nc.vector.memset(xs_window[:].bitcast(I32), 0)
         warm = sb("warm", [P, 1], F32)
         nc.vector.memset(warm[:], 0.0)
-        nc.vector.memset(gs_window[0:GAIN_ROW, : T - 1].bitcast(I32), 0)
-        nc.vector.memset(gs_window[0:GAIN_ROW, T - 1 :].bitcast(I32), 0)
+        nc.vector.memset(gs_window[0:GAIN_ROW, :].bitcast(I32), 0)
+        for q in range(4):
+            nc.scalar.dma_start(
+                xs_window[32 * q : 32 * q + 8, :].bitcast(I32), x_scales[:, 4 * q : 4 * q + 4, :].bitcast(I32)
+            )
+
         nc.scalar.activation(warm[:], warm[:], ACT.Gelu_apprx_tanh)
+
         wsum_bank = bank(7, "wsum_bank")
         for t in range(PACK):
             nc.tensor.transpose(
@@ -131,16 +132,16 @@ def tile_picked_zdq_mlpgelu_po_kernel(
         w1_codes = [sb("w1_codes%d" % o, [P, H], U32) for o in range(2)]
         w1_scales = [sb("w1_scales%d" % o, [P, H], U8) for o in range(2)]
 
-        def quantize_w1(n, split, grouped):
+        def round_w1(copy, n, grouped, first, last):
             o, a, b = w1_pieces[n]
-            if split > 0:
-                dst, src = interleave_views(grouped[:, :split, :], w1_raw[n][:, :, :split])
-                nc.scalar.copy(dst, src)
-            if split < b - a:
-                dst, src = interleave_views(grouped[:, split:, :], w1_raw[n][:, :, split:])
-                nc.vector.tensor_copy(dst, src)
+            copy(
+                grouped[:, :, (a + first) // PACK : (a + last) // PACK, :].rearrange("p (u e) m r -> p u m r e", e=2),
+                w1_raw[n][:, :, first:last].rearrange("p r (m u e) -> p u m r e", u=2, e=2),
+            )
+
+        def quantize_w1(o, grouped):
             nc.vector.quantize_mx(
-                w1_codes[o][:, a:b].bitcast(FP8X4), w1_scales[o][:, a:b], grouped[:].rearrange("p c t -> p (c t)")
+                w1_codes[o][:].bitcast(FP8X4), w1_scales[o][:], grouped[:].rearrange("p t m r -> p (t m r)")
             )
 
         term_at = {0: 38 * KB, 1: 40 * KB, 2: 15 * KB, 3: 17 * KB, 4: 19 * KB, 5: 21 * KB, 6: 32 * KB + 512, 7: 34 * KB + 512}
@@ -152,7 +153,9 @@ def tile_picked_zdq_mlpgelu_po_kernel(
 
         for j in range(2):
             make_offset_term(j)
-        quantize_w1(0, H, sb("w1_grouped0", [P, H, PACK], BF16, "gs_picked"))
+        grouped0 = sb("w1_grouped0", [P, PACK, P, PACK], BF16, "gs_picked")
+        round_w1(nc.scalar.copy, 0, grouped0, 0, H)
+        quantize_w1(0, grouped0)
         for j in range(2, TILES - 2):
             make_offset_term(j)
 
@@ -179,16 +182,18 @@ def tile_picked_zdq_mlpgelu_po_kernel(
                 x1_picked[:, half * 512 : (half + 1) * 512],
                 x1_window[:].bitcast(U32).indirect(offsets[:, 32 * half : 32 * half + 32]),
             )
-        quantize_w1(1, H // 2, placed("w1_grouped1", [P, H // 2, PACK], BF16, 23 * KB))
-        quantize_w1(2, 96, placed("w1_grouped2", [P, H // 2, PACK], BF16, 26 * KB))
+        grouped1 = sb("w1_grouped1", [P, PACK, P, PACK], BF16)
+        round_w1(nc.scalar.copy, 1, grouped1, 0, H // 2)
+        round_w1(nc.scalar.copy, 2, grouped1, 0, 96)
+        round_w1(nc.vector.tensor_copy, 2, grouped1, 96, H // 2)
+        quantize_w1(1, grouped1)
         w2s = placed("w2s", [P, PACK, P], U8, 32 * KB)
         nc.vector.tensor_copy(w2s[:], w2s_raw[:].rearrange("p (m t) -> p t m", t=PACK))
         for j in range(TILES - 2, TILES):
             make_offset_term(j)
 
-        for j in range(8):
-            first_layer(j, w1_pieces[1], x1_picked)
-            first_layer(j, w1_pieces[2], x1_picked)
+        for j in range(6):
+            first_layer(j, (1, 0, H), x1_picked)
 
         out_codes = sb("out_codes", [P, S], I32)
         out_scales = sb("out_scales", [P, S], U8)
@@ -200,12 +205,12 @@ def tile_picked_zdq_mlpgelu_po_kernel(
         result = [sb("result%d" % u, [P, PACK, UNIT], F32) for u in range(units)]
 
         def hidden(j):
-            if j >= 8:
+            if j >= 6:
                 first_layer(j, (1, 0, H), x1_picked)
             pre = sb("pre%d" % j, [P, PACK, P], F32)
-            y_dealt = y_banks[j][:].rearrange("p (m t) -> p t m", t=PACK)
+            y_dealt = y_banks[j][:].rearrange("p (t m) -> p t m", t=PACK)
             term = offset_term[j][:].rearrange("p (t m) -> p t m", t=PACK)
-            added_in_psum = j in ()
+            added_in_psum = j in (2,)
             if added_in_psum:
                 nc.scalar.activation(pre[:], y_dealt, ACT.Copy, scale=gs_cols[:, j, 0:1])
             else:
@@ -264,15 +269,15 @@ def tile_picked_zdq_mlpgelu_po_kernel(
         hidden(3)
         hidden(4)
         hidden(5)
-        second_layer(0)
-        leave(0, (nc.scalar.copy, nc.scalar.copy))
         hidden(6)
-        second_layer(1)
-        leave(1, (nc.vector.tensor_copy, nc.vector.tensor_copy))
         hidden(7)
         second_layer(3)
-        second_layer(2)
+        second_layer(0)
+        second_layer(1)
+        leave(0, (nc.scalar.copy, nc.vector.tensor_copy))
         planes(0, nc.vector.tensor_copy)
+        second_layer(2)
+        leave(1, (nc.scalar.copy, nc.vector.tensor_copy))
         leave(2, (nc.scalar.copy, nc.scalar.copy))
         leave(3, (nc.scalar.copy, nc.scalar.copy))
         planes(1, nc.vector.tensor_copy)

@@ -73,28 +73,27 @@ def tile_picked_zdq_mlpgelu_po_kernel(
             nc.sync.dma_start(raw[:], w1_rows[o, :, :, a:b])
             return raw
 
+        w1_raw = [load_w1(0, placed("w1_raw0", [P, PACK, H], F32, 16 * KB))]
         x0_window = load_x(0, sb("x0_window", [P, T], I32))
 
         ident = sb("ident", [P, P], F32)
         make_identity(nc, ident[:])
         xs_window = sb("xs_window", [P, T], U8)
         nc.vector.memset(xs_window[:].bitcast(I32), 0)
-        warm = sb("warm", [P, 1], F32)
-        nc.vector.memset(warm[:], 0.0)
+        warm = placed("warm", [P, 15 * KB // 4], F32, 29 * KB + 512)
+        nc.vector.memset(warm[:, 0:1], 0.0)
         nc.vector.memset(gs_window[0:GAIN_ROW, :].bitcast(I32), 0)
-        for q in range(4):
-            nc.scalar.dma_start(
-                xs_window[32 * q : 32 * q + 8, :].bitcast(I32), x_scales[:, 4 * q : 4 * q + 4, :].bitcast(I32)
-            )
+        for r in range(4):
+            for o in range(2):
+                nc.scalar.dma_start(xs_window[4 * o + r : P : 32, :].bitcast(I32), x_scales[o, r::4, :].bitcast(I32))
 
-        nc.scalar.activation(warm[:], warm[:], ACT.Gelu_apprx_tanh)
+        nc.scalar.activation(warm[:, 0:1], warm[:, 0:1], ACT.Gelu_apprx_tanh)
 
         wsum_bank = bank(7, "wsum_bank")
         for t in range(PACK):
             nc.tensor.transpose(
                 wsum_bank[:, t * P : (t + 1) * P], wsum_cols[:, t : t + 1].to_broadcast([P, P]), ident[:]
             )
-        w1_raw = [load_w1(0, placed("w1_raw0", [P, PACK, H], F32, 16 * KB))]
         wsum_rows = sb("wsum_rows", [P, H], F32)
         nc.scalar.copy(wsum_rows[:], wsum_bank[:])
 
@@ -104,10 +103,10 @@ def tile_picked_zdq_mlpgelu_po_kernel(
         nc.vector.tensor_copy(
             w2_codes[:].rearrange("p t (m b) -> p t m b", b=2), w2_raw[:].rearrange("p (m t b) -> p t m b", t=PACK, b=2)
         )
-        x1_window = load_x(1, sb("x1_window", [P, T], I32))
+        x1_window = load_x(1, placed("x1_window", [P, T], I32, 44 * KB))
         w1_raw.append(load_w1(1, placed("w1_raw1", [P, PACK, H // 2], F32, 26 * KB)))
         w1_raw.append(load_w1(2, placed("w1_raw2", [P, PACK, H // 2], F32, 32 * KB)))
-        w2s_raw = sb("w2s_raw", [P, N], U8)
+        w2s_raw = placed("w2s_raw", [P, N], U8, 30 * KB)
         nc.vector.memset(w2s_raw[:].bitcast(I32), 0)
         for q in range(4):
             nc.sync.dma_start(
@@ -144,20 +143,17 @@ def tile_picked_zdq_mlpgelu_po_kernel(
                 w1_codes[o][:].bitcast(FP8X4), w1_scales[o][:], grouped[:].rearrange("p t m r -> p (t m r)")
             )
 
-        term_at = {0: 38 * KB, 1: 40 * KB, 2: 15 * KB, 3: 17 * KB, 4: 19 * KB, 5: 21 * KB, 6: 32 * KB + 512, 7: 34 * KB + 512}
         offset_term = {}
 
         def make_offset_term(j):
-            offset_term[j] = placed("offset_term%d" % j, [P, H], F32, term_at[j])
+            offset_term[j] = sb("offset_term%d" % j, [P, H], F32)
             nc.scalar.activation(offset_term[j][:], wsum_rows[:], ACT.Copy, scale=gs_cols[:, j, 1:2])
 
-        for j in range(2):
+        for j in range(8):
             make_offset_term(j)
         grouped0 = sb("w1_grouped0", [P, PACK, P, PACK], BF16, "gs_picked")
         round_w1(nc.scalar.copy, 0, grouped0, 0, H)
         quantize_w1(0, grouped0)
-        for j in range(2, TILES - 2):
-            make_offset_term(j)
 
         y_banks = [bank(j, "y_bank%d" % j) for j in range(TILES)]
 
@@ -189,8 +185,6 @@ def tile_picked_zdq_mlpgelu_po_kernel(
         quantize_w1(1, grouped1)
         w2s = placed("w2s", [P, PACK, P], U8, 32 * KB)
         nc.vector.tensor_copy(w2s[:], w2s_raw[:].rearrange("p (m t) -> p t m", t=PACK))
-        for j in range(TILES - 2, TILES):
-            make_offset_term(j)
 
         for j in range(6):
             first_layer(j, (1, 0, H), x1_picked)

@@ -39,80 +39,92 @@ def tile_picked_zdq_mlpgelu_po_kernel(
     nc = tc.nc
     with ExitStack() as ctx:
         keep = ctx.enter_context(tc.tile_pool(name="keep", bufs=1))
-        reuse = ctx.enter_context(tc.tile_pool(name="reuse", bufs=1))
         psum = ctx.enter_context(tc.psum_pool(name="psum", bufs=1))
 
         def sb(name, shape, dtype, tag=None):
             return keep.tile(shape, dtype, name=name, tag=tag or name, align_bytes=64)
-
-        def placed(name, shape, dtype, offset):
-            return reuse.tile(shape, dtype, name=name, align_bytes=64, offset=offset)
 
         def bank(index, name):
             return psum.tile([P, 512], F32, name=name, tag="bank%d" % index)
 
         offsets = keep.tile([P, S // 16], U16, name="offsets")
         nc.sync.dma_start(offsets[:], offs)
-        gs_window = placed("gs_window", [P, T], F32, 0)
-        nc.scalar.dma_start(gs_window[GAIN_ROW : GAIN_ROW + 1, :], gain[0:1, :])
+        gs_window = sb("gs_window", [P, T], F32)
+        nc.sync.dma_start(gs_window[GAIN_ROW : GAIN_ROW + 1, :], gain[0:1, :])
         nc.sync.dma_start(gs_window[GAIN_ROW + 1 : P, :], shift[0:1, :])
-        wsum_cols = sb("wsum_cols", [P, PACK], F32)
-        nc.sync.dma_start(wsum_cols[:], wsum.rearrange("(p t) o -> p (t o)", t=PACK))
-        w2_raw = sb("w2_raw", [P, 2 * N], U8)
-        nc.sync.dma_start(w2_raw[:].bitcast(I32), w2_words[0].bitcast(I32))
+
+        xs_window = sb("xs_window", [P, T], U8)
+        nc.vector.memset(xs_window[:].bitcast(I32), 0)
+        warm = sb("warm", [P, 1], F32)
+        nc.vector.memset(warm[:], 0.0)
+        w2s_raw = sb("w2s_raw", [P, N], U8)
+        nc.vector.memset(w2s_raw[:].bitcast(I32), 0)
+        ident = sb("ident", [P, P], F32)
+        make_identity(nc, ident[:])
+        nc.gpsimd.memset(gs_window[0:GAIN_ROW, :].bitcast(I32), 0)
 
         w1_rows = w1.rearrange("(o p t) c -> o p t c", p=P, t=PACK)
-        w1_pieces = [(0, 0, H), (1, 0, H // 2), (1, H // 2, H)]
+        w1_pieces = [(0, 0, H), (1, 0, H)]
 
-        def load_x(o, window):
+        def load_x_scales(first, last):
+            for o, r in [divmod(n, 4) for n in range(first, last)]:
+                nc.sync.dma_start(xs_window[4 * o + r : P : 32, :].bitcast(I32), x_scales[o, r::4, :].bitcast(I32))
+
+        def load_x(o):
+            window = sb("x_window%d" % o, [P, T], I32)
             nc.sync.dma_start(window[:], x_words[o].rearrange("p n t -> p (n t)").bitcast(I32))
             return window
 
-        def load_w1(n, raw):
+        def load_w1(n):
             o, a, b = w1_pieces[n]
+            raw = sb("w1_raw%d" % n, [P, PACK, b - a], F32)
             nc.sync.dma_start(raw[:], w1_rows[o, :, :, a:b])
             return raw
 
-        w1_raw = [load_w1(0, placed("w1_raw0", [P, PACK, H], F32, 16 * KB))]
-        x0_window = load_x(0, sb("x0_window", [P, T], I32))
+        nc.scalar.activation(warm[:], warm[:], ACT.Gelu_apprx_tanh)
+        wsum_cols = sb("wsum_cols", [P, PACK], F32)
+        nc.sync.dma_start(wsum_cols[:], wsum.rearrange("(p t) o -> p (t o)", t=PACK))
+        w1_raw = [load_w1(0)]
+        load_x_scales(0, 4)
+        w1_raw.append(load_w1(1))
+        load_x_scales(4, 8)
+        x_window = [load_x(0)]
+        w2_raw = sb("w2_raw", [P, 2 * N], U8)
+        nc.sync.dma_start(w2_raw[:].bitcast(I32), w2_words[0].bitcast(I32))
+        for q in range(4):
+            nc.sync.dma_start(
+                w2s_raw[32 * q : 32 * q + 4, :].bitcast(I32), w2_scales[0, 4 * q : 4 * q + 4, :].bitcast(I32)
+            )
+        x_window.append(load_x(1))
 
-        ident = sb("ident", [P, P], F32)
-        make_identity(nc, ident[:])
-        xs_window = sb("xs_window", [P, T], U8)
-        nc.vector.memset(xs_window[:].bitcast(I32), 0)
-        warm = placed("warm", [P, 15 * KB // 4], F32, 29 * KB + 512)
-        nc.vector.memset(warm[:, 0:1], 0.0)
-        nc.vector.memset(gs_window[0:GAIN_ROW, :].bitcast(I32), 0)
-        for r in range(4):
-            for o in range(2):
-                nc.scalar.dma_start(xs_window[4 * o + r : P : 32, :].bitcast(I32), x_scales[o, r::4, :].bitcast(I32))
+        gs_picked = sb("gs_picked", [P, S], F32)
+        nc.vector.tensor_copy(gs_picked[:], gs_window[:].indirect(offsets[:]))
 
-        nc.scalar.activation(warm[:, 0:1], warm[:, 0:1], ACT.Gelu_apprx_tanh)
+        w1_codes, w1_scales = {}, {}
+
+        def prepare_w1(n):
+            o, a, b = w1_pieces[n]
+            grouped = sb("w1_grouped%d" % n, [P, b - a, PACK], BF16)
+            dst, src = interleave_views(grouped[:], w1_raw[n][:])
+            nc.scalar.copy(dst, src)
+            w1_codes[n] = sb("w1_codes%d" % n, [P, b - a], U32, "xs_window" if n == 1 else None)
+            w1_scales[n] = sb("w1_scales%d" % n, [P, b - a], U8)
+            nc.vector.quantize_mx(w1_codes[n][:].bitcast(FP8X4), w1_scales[n][:], grouped[:].rearrange("p c r -> p (c r)"))
+
+        prepare_w1(0)
+        xs_picked = sb("xs_picked", [P, S], U8)
+        nc.vector.tensor_copy(xs_picked[:], xs_window[:].indirect(offsets[:]))
+        prepare_w1(1)
 
         wsum_bank = bank(7, "wsum_bank")
         for t in range(PACK):
             nc.tensor.transpose(
                 wsum_bank[:, t * P : (t + 1) * P], wsum_cols[:, t : t + 1].to_broadcast([P, P]), ident[:]
             )
-        wsum_rows = sb("wsum_rows", [P, H], F32)
+        wsum_rows = sb("wsum_rows", [P, H], F32, "w1_raw0")
         nc.scalar.copy(wsum_rows[:], wsum_bank[:])
 
-        gs_picked = sb("gs_picked", [P, S], F32)
-        nc.vector.tensor_copy(gs_picked[:], gs_window[:].indirect(offsets[:]))
-        w2_codes = sb("w2_codes", [P, PACK, 2 * P], U8)
-        nc.vector.tensor_copy(
-            w2_codes[:].rearrange("p t (m b) -> p t m b", b=2), w2_raw[:].rearrange("p (m t b) -> p t m b", t=PACK, b=2)
-        )
-        x1_window = load_x(1, placed("x1_window", [P, T], I32, 44 * KB))
-        w1_raw.append(load_w1(1, placed("w1_raw1", [P, PACK, H // 2], F32, 26 * KB)))
-        w1_raw.append(load_w1(2, placed("w1_raw2", [P, PACK, H // 2], F32, 32 * KB)))
-        w2s_raw = placed("w2s_raw", [P, N], U8, 30 * KB)
-        nc.vector.memset(w2s_raw[:].bitcast(I32), 0)
-        for q in range(4):
-            nc.sync.dma_start(
-                w2s_raw[32 * q : 32 * q + 4, :].bitcast(I32), w2_scales[0, 4 * q : 4 * q + 4, :].bitcast(I32)
-            )
-        gs_cols = sb("gs_cols", [P, TILES, 2], F32)
+        gs_cols = sb("gs_cols", [P, TILES, 2], F32, "w1_raw1")
         for half in range(2):
             gs_bank = bank(5 + half, "gs_bank%d" % half)
             for n in range(4):
@@ -123,112 +135,97 @@ def tile_picked_zdq_mlpgelu_po_kernel(
                 gs_bank[:].rearrange("p (n c) -> p n c", n=4)[:, :, GAIN_ROW:P],
             )
 
-        xs_picked = placed("xs_picked", [P, S], U8, 4 * KB)
-        nc.vector.tensor_copy(xs_picked[:], xs_window[:].indirect(offsets[:]))
-        x0_picked = placed("x0_picked", [P, S], U32, 0)
-        nc.vector.tensor_copy(x0_picked[:], x0_window[:].bitcast(U32).indirect(offsets[:]))
-
-        w1_codes = [sb("w1_codes%d" % o, [P, H], U32) for o in range(2)]
-        w1_scales = [sb("w1_scales%d" % o, [P, H], U8) for o in range(2)]
-
-        def round_w1(copy, n, grouped, first, last):
-            o, a, b = w1_pieces[n]
-            copy(
-                grouped[:, :, (a + first) // PACK : (a + last) // PACK, :].rearrange("p (u e) m r -> p u m r e", e=2),
-                w1_raw[n][:, :, first:last].rearrange("p r (m u e) -> p u m r e", u=2, e=2),
+        offset_term = []
+        for j in range(TILES):
+            offset_term.append(sb("offset_term%d" % j, [P, PACK, P], F32))
+            nc.scalar.activation(
+                offset_term[j][:].rearrange("p t m -> p (t m)"), wsum_rows[:], ACT.Copy, scale=gs_cols[:, j, 1:2]
             )
 
-        def quantize_w1(o, grouped):
-            nc.vector.quantize_mx(
-                w1_codes[o][:].bitcast(FP8X4), w1_scales[o][:], grouped[:].rearrange("p t m r -> p (t m r)")
-            )
-
-        offset_term = {}
-
-        def make_offset_term(j):
-            offset_term[j] = sb("offset_term%d" % j, [P, H], F32)
-            nc.scalar.activation(offset_term[j][:], wsum_rows[:], ACT.Copy, scale=gs_cols[:, j, 1:2])
-
-        for j in range(8):
-            make_offset_term(j)
-        grouped0 = sb("w1_grouped0", [P, PACK, P, PACK], BF16, "gs_picked")
-        round_w1(nc.scalar.copy, 0, grouped0, 0, H)
-        quantize_w1(0, grouped0)
 
         y_banks = [bank(j, "y_bank%d" % j) for j in range(TILES)]
+        x_picked = {}
 
-        def first_layer(j, n, codes):
-            o, a, b = n
+        def gather_x(o, half):
+            x_picked[o, half] = sb("x_picked%d_%d" % (o, half), [P, S // 2], U32)
+            nc.vector.tensor_copy(
+                x_picked[o, half][:], x_window[o][:].bitcast(U32).indirect(offsets[:, 32 * half : 32 * half + 32])
+            )
+
+        def first_layer(j, n):
+            o, a, b = w1_pieces[n]
             nc.tensor.matmul_mx(
                 y_banks[j][:, a:b],
-                lhsT=codes[:, j * P : (j + 1) * P].bitcast(FP8X4),
+                lhsT=x_picked[o, j // 4][:, (j % 4) * P : (j % 4 + 1) * P].bitcast(FP8X4),
                 lhsT_scale=xs_picked[4 * o : P, j * P : (j + 1) * P],
-                rhs=w1_codes[o][:, a:b].bitcast(FP8X4),
-                rhs_scale=w1_scales[o][:, a:b],
-                start=(o == 0),
-                stop=(b == H and o == 1),
+                rhs=w1_codes[n][:].bitcast(FP8X4),
+                rhs_scale=w1_scales[n][:],
+                start=(n == 0),
+                stop=(n == 1),
             )
 
-        for j in range(TILES):
-            first_layer(j, (0, 0, H), x0_picked)
-
-        x1_picked = sb("x1_picked", [P, S], U32, "gs_picked")
         for half in range(2):
-            nc.vector.tensor_copy(
-                x1_picked[:, half * 512 : (half + 1) * 512],
-                x1_window[:].bitcast(U32).indirect(offsets[:, 32 * half : 32 * half + 32]),
-            )
-        grouped1 = sb("w1_grouped1", [P, PACK, P, PACK], BF16)
-        round_w1(nc.scalar.copy, 1, grouped1, 0, H // 2)
-        round_w1(nc.scalar.copy, 2, grouped1, 0, 96)
-        round_w1(nc.vector.tensor_copy, 2, grouped1, 96, H // 2)
-        quantize_w1(1, grouped1)
-        w2s = placed("w2s", [P, PACK, P], U8, 32 * KB)
+            gather_x(0, half)
+            for j in range(4 * half, 4 * half + 4):
+                first_layer(j, 0)
+
+        w2_codes = sb("w2_codes", [P, PACK, 2 * P], U8)
+        nc.vector.tensor_copy(
+            w2_codes[:].rearrange("p t (m b) -> p t m b", b=2), w2_raw[:].rearrange("p (m t b) -> p t m b", t=PACK, b=2)
+        )
+        w2s = sb("w2s", [P, PACK, P], U8)
         nc.vector.tensor_copy(w2s[:], w2s_raw[:].rearrange("p (m t) -> p t m", t=PACK))
 
-        for j in range(6):
-            first_layer(j, (1, 0, H), x1_picked)
+        gather_x(1, 0)
+        for j in range(4):
+            first_layer(j, 1)
+        gather_x(1, 1)
 
         out_codes = sb("out_codes", [P, S], I32)
         out_scales = sb("out_scales", [P, S], U8)
         out_rows = out_0.rearrange("(p t) j -> p t j", t=PACK)
         out_words = out_1[0].rearrange("p j r -> p (j r)").bitcast(I32)
-        units = S // UNIT
-        h_grouped = [sb("h_grouped%d" % u, [P, UNIT, PACK], BF16) for u in range(units)]
+        units = [(0, 2), (2, 4), (4, 6), (6, 7), (7, 8)]
+        unit_of = {j: u for u, (a, b) in enumerate(units) for j in range(a, b)}
+        h_grouped = [sb("h_grouped%d" % u, [P, (b - a) * P, PACK], BF16) for u, (a, b) in enumerate(units)]
+        result = [sb("result%d" % u, [P, PACK, (b - a) * P], F32) for u, (a, b) in enumerate(units)]
         out_banks = {}
-        result = [sb("result%d" % u, [P, PACK, UNIT], F32) for u in range(units)]
+        pre = {}
+        on_scalar = (0,)
+
+        def scale(j):
+            pre[j] = sb("pre%d" % j, [P, PACK, P], F32)
+            y_dealt = y_banks[j][:].rearrange("p (m t) -> p t m", t=PACK)
+            if j in on_scalar:
+                nc.scalar.activation(pre[j][:], y_dealt, ACT.Copy, scale=gs_cols[:, j, 0:1])
+            else:
+                nc.vector.scalar_tensor_tensor(pre[j][:], y_dealt, gs_cols[:, j, 0:1], offset_term[j][:], MULT, ADD)
 
         def hidden(j):
-            if j >= 6:
-                first_layer(j, (1, 0, H), x1_picked)
-            pre = sb("pre%d" % j, [P, PACK, P], F32)
-            y_dealt = y_banks[j][:].rearrange("p (t m) -> p t m", t=PACK)
-            term = offset_term[j][:].rearrange("p (t m) -> p t m", t=PACK)
-            added_in_psum = j in (2,)
-            if added_in_psum:
-                nc.scalar.activation(pre[:], y_dealt, ACT.Copy, scale=gs_cols[:, j, 0:1])
-            else:
-                nc.vector.scalar_tensor_tensor(pre[:], y_dealt, gs_cols[:, j, 0:1], term, MULT, ADD)
             turned = bank(j, "turned%d" % j)
             for t in range(PACK):
                 out = turned[:, t * P : (t + 1) * P]
-                nc.tensor.matmul(out, pre[:, t, :], ident[:], start=True, stop=not added_in_psum, is_transpose=True)
-                if added_in_psum:
-                    nc.tensor.matmul(out, term[:, t, :], ident[:], start=False, stop=True, is_transpose=True)
+                nc.tensor.matmul(out, pre[j][:, t, :], ident[:], start=True, stop=j not in on_scalar, is_transpose=True)
+                if j in on_scalar:
+                    nc.tensor.matmul(out, offset_term[j][:, t, :], ident[:], start=False, stop=True, is_transpose=True)
+            place = j - units[unit_of[j]][0]
             nc.scalar.activation(
-                h_grouped[j // 2][:, (j % 2) * P : (j % 2 + 1) * P, :],
+                h_grouped[unit_of[j]][:, place * P : (place + 1) * P, :],
                 turned[:].rearrange("p (t j) -> p j t", t=PACK),
                 ACT.Gelu_apprx_tanh,
             )
 
         def second_layer(u):
-            h_codes = sb("h_codes%d" % u, [P, UNIT], U32)
-            h_scales = sb("h_scales%d" % u, [P, UNIT], U8)
+            a, b = units[u]
+            width = (b - a) * P
+            h_codes = sb("h_codes%d" % u, [P, width], U32)
+            h_scales = sb("h_scales%d" % u, [P, width], U8)
             nc.vector.quantize_mx(h_codes[:].bitcast(FP8X4), h_scales[:], h_grouped[u][:].rearrange("p j t -> p (j t)"))
-            out_banks[u] = [bank(2 * u + n, "out_bank%d" % (2 * u + n)) for n in range(2)]
+            out_banks[u] = [bank(j, "out_bank%d" % j) for j in range(a, b)]
             for t in range(PACK):
+                n, place = divmod(t * width, 512)
                 nc.tensor.matmul_mx(
-                    out_banks[u][t // 2][:, (t % 2) * UNIT : (t % 2 + 1) * UNIT],
+                    out_banks[u][n][:, place : place + width],
                     lhsT=w2_codes[:, t, :].bitcast(FP4X4),
                     lhsT_scale=w2s[:, t, :],
                     rhs=h_codes[:].bitcast(FP8X4),
@@ -238,45 +235,61 @@ def tile_picked_zdq_mlpgelu_po_kernel(
                 )
 
         def leave(u, copies):
-            for n in range(2):
-                copies[n](result[u][:, 2 * n : 2 * n + 2, :].rearrange("p t j -> p (t j)"), out_banks[u][n][:])
-                nc.sync.dma_start(
-                    out_rows[:, 2 * n : 2 * n + 2, u * UNIT : (u + 1) * UNIT], result[u][:, 2 * n : 2 * n + 2, :]
-                )
+            a, b = units[u]
+            rows = PACK // (b - a)
+            for n in range(b - a):
+                part = result[u][:, rows * n : rows * (n + 1), :]
+                copies[n](part.rearrange("p t j -> p (t j)"), out_banks[u][n][:])
+                nc.sync.dma_start(out_rows[:, rows * n : rows * (n + 1), a * P : b * P], part)
 
         def planes(u, copy):
-            out_grouped = sb("out_grouped%d" % u, [P, UNIT, PACK], BF16)
+            a, b = units[u]
+            out_grouped = sb("out_grouped%d" % u, [P, (b - a) * P, PACK], BF16)
             dst, src = interleave_views(out_grouped[:], result[u][:])
             copy(dst, src)
-            cols = slice(u * UNIT, (u + 1) * UNIT)
+            cols = slice(a * P, b * P)
             nc.vector.quantize_mx(
                 out_codes[:, cols].bitcast(FP8X4), out_scales[:, cols], out_grouped[:].rearrange("p j t -> p (j t)")
             )
-            if u == units - 2:
-                nc.sync.dma_start(out_words[:, : S - UNIT], out_codes[:, : S - UNIT])
-            if u == units - 1:
-                nc.scalar.dma_start(out_words[:, cols], out_codes[:, cols])
+            if u == 2:
+                nc.sync.dma_start(out_words[:, : b * P], out_codes[:, : b * P])
+            if u == len(units) - 1:
+                nc.scalar.dma_start(out_words[:, 6 * P :], out_codes[:, 6 * P :])
 
+        V, A = nc.vector.tensor_copy, nc.scalar.copy
+        for j in range(4):
+            scale(j)
+        first_layer(4, 1)
+        first_layer(5, 1)
         hidden(0)
         hidden(1)
+        first_layer(6, 1)
+        scale(4)
+        scale(5)
         hidden(2)
         hidden(3)
+        first_layer(7, 1)
+        scale(6)
+        second_layer(0)
+        scale(7)
         hidden(4)
         hidden(5)
+        second_layer(1)
         hidden(6)
         hidden(7)
-        second_layer(3)
-        second_layer(0)
-        second_layer(1)
-        leave(0, (nc.scalar.copy, nc.vector.tensor_copy))
-        planes(0, nc.vector.tensor_copy)
         second_layer(2)
-        leave(1, (nc.scalar.copy, nc.vector.tensor_copy))
-        leave(2, (nc.scalar.copy, nc.scalar.copy))
-        leave(3, (nc.scalar.copy, nc.scalar.copy))
-        planes(1, nc.vector.tensor_copy)
-        planes(2, nc.vector.tensor_copy)
-        planes(3, nc.vector.tensor_copy)
+        second_layer(3)
+        second_layer(4)
+        leave(0, (V, V))
+        leave(1, (A, A))
+        planes(0, V)
+        leave(2, (A, A))
+        planes(1, V)
+        leave(3, (A,))
+        leave(4, (A,))
+        planes(2, V)
+        planes(3, V)
+        planes(4, V)
         for q in range(4):
             engine = nc.sync if q < 3 else nc.scalar
             engine.dma_start(

@@ -51,24 +51,23 @@ def tile_picked_zdq_mlpgelu_po_kernel(
         nc.sync.dma_start(offsets[:], offs)
         gs_window = sb("gs_window", [P, T], F32)
         nc.sync.dma_start(gs_window[GAIN_ROW : GAIN_ROW + 1, :], gain[0:1, :])
-        nc.sync.dma_start(gs_window[GAIN_ROW + 1 : P, :], shift[0:1, :])
 
         xs_window = sb("xs_window", [P, T], U8)
         nc.vector.memset(xs_window[:].bitcast(I32), 0)
+        nc.vector.memset(gs_window[0:GAIN_ROW, :].bitcast(I32), 0)
         warm = sb("warm", [P, 1], F32)
         nc.vector.memset(warm[:], 0.0)
         w2s_raw = sb("w2s_raw", [P, N], U8)
         nc.vector.memset(w2s_raw[:].bitcast(I32), 0)
         ident = sb("ident", [P, P], F32)
         make_identity(nc, ident[:])
-        nc.gpsimd.memset(gs_window[0:GAIN_ROW, :].bitcast(I32), 0)
+        for r in range(4):
+            for o in range(2):
+                nc.scalar.dma_start(xs_window[4 * o + r : P : 32, :].bitcast(I32), x_scales[o, r::4, :].bitcast(I32))
+        nc.scalar.activation(warm[:], warm[:], ACT.Gelu_apprx_tanh)
 
         w1_rows = w1.rearrange("(o p t) c -> o p t c", p=P, t=PACK)
         w1_pieces = [(0, 0, H), (1, 0, H)]
-
-        def load_x_scales(first, last):
-            for o, r in [divmod(n, 4) for n in range(first, last)]:
-                nc.sync.dma_start(xs_window[4 * o + r : P : 32, :].bitcast(I32), x_scales[o, r::4, :].bitcast(I32))
 
         def load_x(o):
             window = sb("x_window%d" % o, [P, T], I32)
@@ -81,16 +80,14 @@ def tile_picked_zdq_mlpgelu_po_kernel(
             nc.sync.dma_start(raw[:], w1_rows[o, :, :, a:b])
             return raw
 
-        nc.scalar.activation(warm[:], warm[:], ACT.Gelu_apprx_tanh)
+        w1_raw = [load_w1(0)]
+        nc.sync.dma_start(gs_window[GAIN_ROW + 1 : P, :], shift[0:1, :])
+        w1_raw.append(load_w1(1))
         wsum_cols = sb("wsum_cols", [P, PACK], F32)
         nc.sync.dma_start(wsum_cols[:], wsum.rearrange("(p t) o -> p (t o)", t=PACK))
-        w1_raw = [load_w1(0)]
-        load_x_scales(0, 4)
-        w1_raw.append(load_w1(1))
-        load_x_scales(4, 8)
-        x_window = [load_x(0)]
         w2_raw = sb("w2_raw", [P, 2 * N], U8)
         nc.sync.dma_start(w2_raw[:].bitcast(I32), w2_words[0].bitcast(I32))
+        x_window = [load_x(0)]
         for q in range(4):
             nc.sync.dma_start(
                 w2s_raw[32 * q : 32 * q + 4, :].bitcast(I32), w2_scales[0, 4 * q : 4 * q + 4, :].bitcast(I32)
@@ -105,9 +102,11 @@ def tile_picked_zdq_mlpgelu_po_kernel(
         def prepare_w1(n):
             o, a, b = w1_pieces[n]
             grouped = sb("w1_grouped%d" % n, [P, b - a, PACK], BF16)
-            dst, src = interleave_views(grouped[:], w1_raw[n][:])
-            nc.scalar.copy(dst, src)
-            w1_codes[n] = sb("w1_codes%d" % n, [P, b - a], U32, "xs_window" if n == 1 else None)
+            nc.scalar.copy(
+                grouped[:].rearrange("p (t m) r -> p m t r", t=PACK),
+                w1_raw[n][:].rearrange("p r (m t) -> p m t r", t=PACK),
+            )
+            w1_codes[n] = sb("w1_codes%d" % n, [P, b - a], U32, "gs_window" if n == 0 else None)
             w1_scales[n] = sb("w1_scales%d" % n, [P, b - a], U8)
             nc.vector.quantize_mx(w1_codes[n][:].bitcast(FP8X4), w1_scales[n][:], grouped[:].rearrange("p c r -> p (c r)"))
 
@@ -121,7 +120,7 @@ def tile_picked_zdq_mlpgelu_po_kernel(
             nc.tensor.transpose(
                 wsum_bank[:, t * P : (t + 1) * P], wsum_cols[:, t : t + 1].to_broadcast([P, P]), ident[:]
             )
-        wsum_rows = sb("wsum_rows", [P, H], F32, "w1_raw0")
+        wsum_rows = sb("wsum_rows", [P, H], F32)
         nc.scalar.copy(wsum_rows[:], wsum_bank[:])
 
         gs_cols = sb("gs_cols", [P, TILES, 2], F32, "w1_raw1")
@@ -195,7 +194,7 @@ def tile_picked_zdq_mlpgelu_po_kernel(
 
         def scale(j):
             pre[j] = sb("pre%d" % j, [P, PACK, P], F32)
-            y_dealt = y_banks[j][:].rearrange("p (m t) -> p t m", t=PACK)
+            y_dealt = y_banks[j][:].rearrange("p (t m) -> p t m", t=PACK)
             if j in on_scalar:
                 nc.scalar.activation(pre[j][:], y_dealt, ACT.Copy, scale=gs_cols[:, j, 0:1])
             else:

@@ -54,17 +54,21 @@ def tile_picked_zdq_mlpgelu_po_kernel(
 
         xs_window = sb("xs_window", [P, T], U8)
         nc.vector.memset(xs_window[:].bitcast(I32), 0)
-        nc.vector.memset(gs_window[0:GAIN_ROW, :].bitcast(I32), 0)
+        nc.sync.dma_start(xs_window[0:P:4, :].bitcast(I32), x_scales.rearrange("o q c -> (o q) c").bitcast(I32))
         warm = sb("warm", [P, 1], F32)
         nc.vector.memset(warm[:], 0.0)
         w2s_raw = sb("w2s_raw", [P, N], U8)
         nc.vector.memset(w2s_raw[:].bitcast(I32), 0)
+        nc.vector.memset(gs_window[0:GAIN_ROW, 0 : T // 2].bitcast(I32), 0)
+        xs_picked = sb("xs_picked", [P, S], U8)
+        nc.vector.memset(xs_picked[:].bitcast(I32), 0)
         ident = sb("ident", [P, P], F32)
         make_identity(nc, ident[:])
-        for r in range(4):
-            for o in range(2):
-                nc.scalar.dma_start(xs_window[4 * o + r : P : 32, :].bitcast(I32), x_scales[o, r::4, :].bitcast(I32))
-        nc.scalar.activation(warm[:], warm[:], ACT.Gelu_apprx_tanh)
+        nc.scalar.activation(
+            gs_window[0:GAIN_ROW, T // 2 : T], warm[0:GAIN_ROW, :].to_broadcast([GAIN_ROW, T // 2]), ACT.Gelu_apprx_tanh
+        )
+        xs_gathered = sb("xs_gathered", [P, S], U8)
+        nc.vector.tensor_copy(xs_gathered[:], xs_window[:].indirect(offsets[:]))
 
         w1_rows = w1.rearrange("(o p t) c -> o p t c", p=P, t=PACK)
         w1_pieces = [(0, 0, H), (1, 0, H)]
@@ -80,18 +84,31 @@ def tile_picked_zdq_mlpgelu_po_kernel(
             nc.sync.dma_start(raw[:], w1_rows[o, :, :, a:b])
             return raw
 
+        def load_w2_scales(first, last):
+            for q in range(first, last):
+                nc.sync.dma_start(
+                    w2s_raw[32 * q : 32 * q + 4, :].bitcast(I32), w2_scales[0, 4 * q : 4 * q + 4, :].bitcast(I32)
+                )
+
+        def move_x_scales(first, last):
+            for r, o in [divmod(n, 2) for n in range(first, last)]:
+                nc.sync.dma_start(
+                    xs_picked[4 * o + r : P : 32, :].bitcast(I32),
+                    xs_gathered[64 * o + 4 * r : 64 * o + 64 : 16, :].bitcast(I32),
+                )
+
         w1_raw = [load_w1(0)]
         nc.sync.dma_start(gs_window[GAIN_ROW + 1 : P, :], shift[0:1, :])
-        w1_raw.append(load_w1(1))
         wsum_cols = sb("wsum_cols", [P, PACK], F32)
         nc.sync.dma_start(wsum_cols[:], wsum.rearrange("(p t) o -> p (t o)", t=PACK))
         w2_raw = sb("w2_raw", [P, 2 * N], U8)
         nc.sync.dma_start(w2_raw[:].bitcast(I32), w2_words[0].bitcast(I32))
+        load_w2_scales(0, 3)
+        w1_raw.append(load_w1(1))
+        load_w2_scales(3, 4)
+        move_x_scales(0, 2)
         x_window = [load_x(0)]
-        for q in range(4):
-            nc.sync.dma_start(
-                w2s_raw[32 * q : 32 * q + 4, :].bitcast(I32), w2_scales[0, 4 * q : 4 * q + 4, :].bitcast(I32)
-            )
+        move_x_scales(2, 8)
         x_window.append(load_x(1))
 
         gs_picked = sb("gs_picked", [P, S], F32)
@@ -99,31 +116,29 @@ def tile_picked_zdq_mlpgelu_po_kernel(
 
         w1_codes, w1_scales = {}, {}
 
-        def prepare_w1(n):
+        def prepare_w1(n, copy):
             o, a, b = w1_pieces[n]
             grouped = sb("w1_grouped%d" % n, [P, b - a, PACK], BF16)
-            nc.scalar.copy(
+            copy(
                 grouped[:].rearrange("p (t m) r -> p m t r", t=PACK),
                 w1_raw[n][:].rearrange("p r (m t) -> p m t r", t=PACK),
             )
-            w1_codes[n] = sb("w1_codes%d" % n, [P, b - a], U32, "gs_window" if n == 0 else None)
+            w1_codes[n] = sb("w1_codes%d" % n, [P, b - a], U32, "w1_raw1" if n == 0 else None)
             w1_scales[n] = sb("w1_scales%d" % n, [P, b - a], U8)
             nc.vector.quantize_mx(w1_codes[n][:].bitcast(FP8X4), w1_scales[n][:], grouped[:].rearrange("p c r -> p (c r)"))
 
-        prepare_w1(0)
-        xs_picked = sb("xs_picked", [P, S], U8)
-        nc.vector.tensor_copy(xs_picked[:], xs_window[:].indirect(offsets[:]))
-        prepare_w1(1)
+        prepare_w1(1, nc.vector.tensor_copy)
+        prepare_w1(0, nc.scalar.copy)
 
         wsum_bank = bank(7, "wsum_bank")
         for t in range(PACK):
             nc.tensor.transpose(
                 wsum_bank[:, t * P : (t + 1) * P], wsum_cols[:, t : t + 1].to_broadcast([P, P]), ident[:]
             )
-        wsum_rows = sb("wsum_rows", [P, H], F32)
+        wsum_rows = sb("wsum_rows", [P, H], F32, "w1_raw0")
         nc.scalar.copy(wsum_rows[:], wsum_bank[:])
 
-        gs_cols = sb("gs_cols", [P, TILES, 2], F32, "w1_raw1")
+        gs_cols = sb("gs_cols", [P, TILES, 2], F32)
         for half in range(2):
             gs_bank = bank(5 + half, "gs_bank%d" % half)
             for n in range(4):
@@ -276,21 +291,21 @@ def tile_picked_zdq_mlpgelu_po_kernel(
         second_layer(1)
         hidden(6)
         hidden(7)
+        leave(0, (V, V))
         second_layer(2)
         second_layer(3)
         second_layer(4)
-        leave(0, (V, V))
-        leave(1, (A, A))
-        planes(0, V)
+        leave(1, (V, A))
         leave(2, (A, A))
-        planes(1, V)
         leave(3, (A,))
         leave(4, (A,))
+        planes(0, V)
+        planes(1, V)
         planes(2, V)
         planes(3, V)
         planes(4, V)
         for q in range(4):
-            engine = nc.sync if q < 3 else nc.scalar
+            engine = nc.sync if q < 2 else nc.scalar
             engine.dma_start(
                 out_2[0, 4 * q : 4 * q + 4, :].bitcast(I32), out_scales[32 * q : 32 * q + 4, :].bitcast(I32)
             )

@@ -39,10 +39,14 @@ def tile_picked_zdq_mlpgelu_po_kernel(
     nc = tc.nc
     with ExitStack() as ctx:
         keep = ctx.enter_context(tc.tile_pool(name="keep", bufs=1))
+        reuse = ctx.enter_context(tc.tile_pool(name="reuse", bufs=1))
         psum = ctx.enter_context(tc.psum_pool(name="psum", bufs=1))
 
         def sb(name, shape, dtype, tag=None):
             return keep.tile(shape, dtype, name=name, tag=tag or name, align_bytes=64)
+
+        def placed(name, shape, dtype, offset):
+            return reuse.tile(shape, dtype, name=name, align_bytes=64, offset=offset)
 
         def bank(index, name):
             return psum.tile([P, 512], F32, name=name, tag="bank%d" % index)
@@ -54,7 +58,6 @@ def tile_picked_zdq_mlpgelu_po_kernel(
 
         xs_window = sb("xs_window", [P, T], U8)
         nc.vector.memset(xs_window[:].bitcast(I32), 0)
-        nc.sync.dma_start(xs_window[0:P:4, :].bitcast(I32), x_scales.rearrange("o q c -> (o q) c").bitcast(I32))
         warm = sb("warm", [P, 1], F32)
         nc.vector.memset(warm[:], 0.0)
         w2s_raw = sb("w2s_raw", [P, N], U8)
@@ -67,16 +70,14 @@ def tile_picked_zdq_mlpgelu_po_kernel(
         nc.scalar.activation(
             gs_window[0:GAIN_ROW, T // 2 : T], warm[0:GAIN_ROW, :].to_broadcast([GAIN_ROW, T // 2]), ACT.Gelu_apprx_tanh
         )
-        xs_gathered = sb("xs_gathered", [P, S], U8)
-        nc.vector.tensor_copy(xs_gathered[:], xs_window[:].indirect(offsets[:]))
 
         w1_rows = w1.rearrange("(o p t) c -> o p t c", p=P, t=PACK)
         w1_pieces = [(0, 0, H), (1, 0, H)]
 
-        def load_x(o):
-            window = sb("x_window%d" % o, [P, T], I32)
-            nc.sync.dma_start(window[:], x_words[o].rearrange("p n t -> p (n t)").bitcast(I32))
-            return window
+        x_window = [placed("x_window0", [P, T], I32, 0), sb("x_window1", [P, T], I32)]
+
+        def load_x(o, a, b):
+            nc.sync.dma_start(x_window[o][:, a:b], x_words[o].rearrange("p n t -> p (n t)").bitcast(I32)[:, a:b])
 
         def load_w1(n):
             o, a, b = w1_pieces[n]
@@ -98,44 +99,52 @@ def tile_picked_zdq_mlpgelu_po_kernel(
                 )
 
         w1_raw = [load_w1(0)]
+        nc.sync.dma_start(xs_window[0:P:4, :].bitcast(I32), x_scales.rearrange("o q c -> (o q) c").bitcast(I32))
         nc.sync.dma_start(gs_window[GAIN_ROW + 1 : P, :], shift[0:1, :])
         wsum_cols = sb("wsum_cols", [P, PACK], F32)
         nc.sync.dma_start(wsum_cols[:], wsum.rearrange("(p t) o -> p (t o)", t=PACK))
         w2_raw = sb("w2_raw", [P, 2 * N], U8)
         nc.sync.dma_start(w2_raw[:].bitcast(I32), w2_words[0].bitcast(I32))
-        load_w2_scales(0, 3)
         w1_raw.append(load_w1(1))
-        load_w2_scales(3, 4)
+        load_w2_scales(0, 4)
+        load_x(0, 0, T // 2)
+        xs_gathered = sb("xs_gathered", [P, S], U8)
+        nc.vector.tensor_copy(xs_gathered[:], xs_window[:].indirect(offsets[:]))
         move_x_scales(0, 2)
-        x_window = [load_x(0)]
+        load_x(0, T // 2, T)
         move_x_scales(2, 8)
-        x_window.append(load_x(1))
+        load_x(1, 0, T)
 
-        gs_picked = sb("gs_picked", [P, S], F32)
+        gs_picked = sb("gs_picked", [P, S], F32, "xs_window")
         nc.vector.tensor_copy(gs_picked[:], gs_window[:].indirect(offsets[:]))
 
-        w1_codes, w1_scales = {}, {}
+        w1_codes = [sb("w1_codes0", [P, H], U32), placed("w1_codes1", [P, H], U32, 0)]
+        w1_scales = {}
+        w1_grouped = [sb("w1_grouped%d" % n, [P, H, PACK], BF16) for n in range(2)]
 
-        def prepare_w1(n, copy):
-            o, a, b = w1_pieces[n]
-            grouped = sb("w1_grouped%d" % n, [P, b - a, PACK], BF16)
+        def prepare_w1(n, copy, first, last):
             copy(
-                grouped[:].rearrange("p (t m) r -> p m t r", t=PACK),
-                w1_raw[n][:].rearrange("p r (m t) -> p m t r", t=PACK),
+                w1_grouped[n][:].rearrange("p (t m) r -> p m t r", t=PACK)[:, first:last],
+                w1_raw[n][:].rearrange("p r (m t) -> p m t r", t=PACK)[:, first:last],
             )
-            w1_codes[n] = sb("w1_codes%d" % n, [P, b - a], U32, "w1_raw1" if n == 0 else None)
-            w1_scales[n] = sb("w1_scales%d" % n, [P, b - a], U8)
-            nc.vector.quantize_mx(w1_codes[n][:].bitcast(FP8X4), w1_scales[n][:], grouped[:].rearrange("p c r -> p (c r)"))
 
-        prepare_w1(1, nc.vector.tensor_copy)
-        prepare_w1(0, nc.scalar.copy)
+        def quantize_w1(n):
+            w1_scales[n] = sb("w1_scales%d" % n, [P, H], U8)
+            nc.vector.quantize_mx(
+                w1_codes[n][:].bitcast(FP8X4), w1_scales[n][:], w1_grouped[n][:].rearrange("p c r -> p (c r)")
+            )
+
+        prepare_w1(0, nc.scalar.copy, 0, P)
+        quantize_w1(0)
+        prepare_w1(1, nc.scalar.copy, 0, P // 2)
+        prepare_w1(1, nc.vector.tensor_copy, P // 2, P)
 
         wsum_bank = bank(7, "wsum_bank")
         for t in range(PACK):
             nc.tensor.transpose(
                 wsum_bank[:, t * P : (t + 1) * P], wsum_cols[:, t : t + 1].to_broadcast([P, P]), ident[:]
             )
-        wsum_rows = sb("wsum_rows", [P, H], F32, "w1_raw0")
+        wsum_rows = sb("wsum_rows", [P, H], F32, "w1_raw1")
         nc.scalar.copy(wsum_rows[:], wsum_bank[:])
 
         gs_cols = sb("gs_cols", [P, TILES, 2], F32)
@@ -183,11 +192,12 @@ def tile_picked_zdq_mlpgelu_po_kernel(
             for j in range(4 * half, 4 * half + 4):
                 first_layer(j, 0)
 
-        w2_codes = sb("w2_codes", [P, PACK, 2 * P], U8)
+        quantize_w1(1)
+        w2_codes = placed("w2_codes", [P, PACK, 2 * P], U8, 4 * KB)
         nc.vector.tensor_copy(
             w2_codes[:].rearrange("p t (m b) -> p t m b", b=2), w2_raw[:].rearrange("p (m t b) -> p t m b", t=PACK, b=2)
         )
-        w2s = sb("w2s", [P, PACK, P], U8)
+        w2s = placed("w2s", [P, PACK, P], U8, 8 * KB)
         nc.vector.tensor_copy(w2s[:], w2s_raw[:].rearrange("p (m t) -> p t m", t=PACK))
 
         gather_x(1, 0)
@@ -256,14 +266,17 @@ def tile_picked_zdq_mlpgelu_po_kernel(
                 copies[n](part.rearrange("p t j -> p (t j)"), out_banks[u][n][:])
                 nc.sync.dma_start(out_rows[:, rows * n : rows * (n + 1), a * P : b * P], part)
 
-        def planes(u, copy):
+        out_grouped = [sb("out_grouped%d" % u, [P, (b - a) * P, PACK], BF16) for u, (a, b) in enumerate(units)]
+
+        def round_result(u):
+            dst, src = interleave_views(out_grouped[u][:], result[u][:])
+            nc.vector.tensor_copy(dst, src)
+
+        def planes(u):
             a, b = units[u]
-            out_grouped = sb("out_grouped%d" % u, [P, (b - a) * P, PACK], BF16)
-            dst, src = interleave_views(out_grouped[:], result[u][:])
-            copy(dst, src)
             cols = slice(a * P, b * P)
             nc.vector.quantize_mx(
-                out_codes[:, cols].bitcast(FP8X4), out_scales[:, cols], out_grouped[:].rearrange("p j t -> p (j t)")
+                out_codes[:, cols].bitcast(FP8X4), out_scales[:, cols], out_grouped[u][:].rearrange("p j t -> p (j t)")
             )
             if u == 2:
                 nc.sync.dma_start(out_words[:, : b * P], out_codes[:, : b * P])
@@ -291,19 +304,19 @@ def tile_picked_zdq_mlpgelu_po_kernel(
         second_layer(1)
         hidden(6)
         hidden(7)
-        leave(0, (V, V))
+        leave(0, (V, A))
         second_layer(2)
         second_layer(3)
         second_layer(4)
-        leave(1, (V, A))
+        leave(1, (A, A))
         leave(2, (A, A))
         leave(3, (A,))
         leave(4, (A,))
-        planes(0, V)
-        planes(1, V)
-        planes(2, V)
-        planes(3, V)
-        planes(4, V)
+        round_result(0)
+        for u in range(1, len(units)):
+            round_result(u)
+            planes(u - 1)
+        planes(len(units) - 1)
         for q in range(4):
             engine = nc.sync if q < 2 else nc.scalar
             engine.dma_start(

@@ -193,7 +193,7 @@ def tile_picked_zdq_mlpgelu_po_kernel(
                 first_layer(j, 0)
 
         quantize_w1(1)
-        w2_codes = placed("w2_codes", [P, PACK, 2 * P], U8, 4 * KB)
+        w2_codes = sb("w2_codes", [P, PACK, 2 * P], U8)
         nc.vector.tensor_copy(
             w2_codes[:].rearrange("p t (m b) -> p t m b", b=2), w2_raw[:].rearrange("p (m t b) -> p t m b", t=PACK, b=2)
         )
@@ -278,10 +278,9 @@ def tile_picked_zdq_mlpgelu_po_kernel(
             nc.vector.quantize_mx(
                 out_codes[:, cols].bitcast(FP8X4), out_scales[:, cols], out_grouped[u][:].rearrange("p j t -> p (j t)")
             )
-            if u == 2:
-                nc.sync.dma_start(out_words[:, : b * P], out_codes[:, : b * P])
-            if u == len(units) - 1:
-                nc.scalar.dma_start(out_words[:, 6 * P :], out_codes[:, 6 * P :])
+            if b % 2 == 0:
+                cols = slice((b - 2) * P, b * P)
+                nc.sync.dma_start(out_words[:, cols], out_codes[:, cols])
 
         V, A = nc.vector.tensor_copy, nc.scalar.copy
         for j in range(4):
@@ -304,11 +303,11 @@ def tile_picked_zdq_mlpgelu_po_kernel(
         second_layer(1)
         hidden(6)
         hidden(7)
-        leave(0, (V, A))
+        leave(0, (V, V))
         second_layer(2)
         second_layer(3)
         second_layer(4)
-        leave(1, (A, A))
+        leave(1, (V, A))
         leave(2, (A, A))
         leave(3, (A,))
         leave(4, (A,))

@@ -298,16 +298,16 @@ def tile_picked_zdq_mlpgelu_po_kernel(
         scale(6)
         second_layer(0)
         scale(7)
+        leave(0, (A, V))
         hidden(4)
         hidden(5)
         second_layer(1)
         hidden(6)
         hidden(7)
-        leave(0, (V, V))
         second_layer(2)
         second_layer(3)
         second_layer(4)
-        leave(1, (V, A))
+        leave(1, (V, V))
         leave(2, (A, A))
         leave(3, (A,))
         leave(4, (A,))

@@ -169,17 +169,17 @@ def tile_picked_zdq_mlpgelu_po_kernel(
         y_banks = [bank(j, "y_bank%d" % j) for j in range(TILES)]
         x_picked = {}
 
-        def gather_x(o, half):
-            x_picked[o, half] = sb("x_picked%d_%d" % (o, half), [P, S // 2], U32)
-            nc.vector.tensor_copy(
-                x_picked[o, half][:], x_window[o][:].bitcast(U32).indirect(offsets[:, 32 * half : 32 * half + 32])
-            )
+        def gather_x(o, first, last, tag=None):
+            picked = sb("x_picked%d_%d" % (o, first), [P, (last - first) * P], U32, tag)
+            nc.vector.tensor_copy(picked[:], x_window[o][:].bitcast(U32).indirect(offsets[:, 8 * first : 8 * last]))
+            for j in range(first, last):
+                x_picked[o, j] = picked[:, (j - first) * P : (j - first + 1) * P]
 
         def first_layer(j, n):
             o, a, b = w1_pieces[n]
             nc.tensor.matmul_mx(
                 y_banks[j][:, a:b],
-                lhsT=x_picked[o, j // 4][:, (j % 4) * P : (j % 4 + 1) * P].bitcast(FP8X4),
+                lhsT=x_picked[o, j].bitcast(FP8X4),
                 lhsT_scale=xs_picked[4 * o : P, j * P : (j + 1) * P],
                 rhs=w1_codes[n][:].bitcast(FP8X4),
                 rhs_scale=w1_scales[n][:],
@@ -188,7 +188,7 @@ def tile_picked_zdq_mlpgelu_po_kernel(
             )
 
         for half in range(2):
-            gather_x(0, half)
+            gather_x(0, 4 * half, 4 * half + 4)
             for j in range(4 * half, 4 * half + 4):
                 first_layer(j, 0)
 
@@ -200,10 +200,11 @@ def tile_picked_zdq_mlpgelu_po_kernel(
         w2s = placed("w2s", [P, PACK, P], U8, 8 * KB)
         nc.vector.tensor_copy(w2s[:], w2s_raw[:].rearrange("p (m t) -> p t m", t=PACK))
 
-        gather_x(1, 0)
-        for j in range(4):
-            first_layer(j, 1)
-        gather_x(1, 1)
+        for first in (0, 2):
+            gather_x(1, first, first + 2)
+            first_layer(first, 1)
+            first_layer(first + 1, 1)
+        gather_x(1, 4, 6)
 
         out_codes = sb("out_codes", [P, S], I32)
         out_scales = sb("out_scales", [P, S], U8)
@@ -283,10 +284,13 @@ def tile_picked_zdq_mlpgelu_po_kernel(
                 nc.sync.dma_start(out_words[:, cols], out_codes[:, cols])
 
         V, A = nc.vector.tensor_copy, nc.scalar.copy
-        for j in range(4):
-            scale(j)
         first_layer(4, 1)
         first_layer(5, 1)
+        scale(0)
+        scale(1)
+        gather_x(1, 6, 8, "offset_term1")
+        scale(2)
+        scale(3)
         hidden(0)
         hidden(1)
         first_layer(6, 1)
@@ -307,7 +311,7 @@ def tile_picked_zdq_mlpgelu_po_kernel(
         second_layer(2)
         second_layer(3)
         second_layer(4)
-        leave(1, (V, V))
+        leave(1, (V, A))
         leave(2, (A, A))
         leave(3, (A,))
         leave(4, (A,))

@@ -21,16 +21,10 @@ ADD = mybir.AluOpType.add
 P = 128
 PACK = 4
 TILES = S // P
-UNIT = 2 * P
-GAIN_ROW = P - 2
+GAIN_ROW, SHIFT_ROW = 126, 127
+FILL_POOL, FILL_SPLIT = 1088, 3339
+X_SPLIT = 3 * T // 4
 KB = 1024
-
-
-def interleave_views(dst, src):
-    return (
-        dst.rearrange("p (c i) t -> p c t i", i=4),
-        src.rearrange("p t (c i) -> p c t i", i=4),
-    )
 
 
 def tile_picked_zdq_mlpgelu_po_kernel(
@@ -53,101 +47,86 @@ def tile_picked_zdq_mlpgelu_po_kernel(
 
         offsets = keep.tile([P, S // 16], U16, name="offsets")
         nc.sync.dma_start(offsets[:], offs)
-        gs_window = sb("gs_window", [P, T], F32)
-        nc.sync.dma_start(gs_window[GAIN_ROW : GAIN_ROW + 1, :], gain[0:1, :])
 
+        zero = sb("zero", [P, 1], F32)
+        nc.vector.memset(zero[:], 0.0)
         xs_window = sb("xs_window", [P, T], U8)
-        nc.vector.memset(xs_window[:].bitcast(I32), 0)
-        warm = sb("warm", [P, 1], F32)
-        nc.vector.memset(warm[:], 0.0)
-        w2s_raw = sb("w2s_raw", [P, N], U8)
-        nc.vector.memset(w2s_raw[:].bitcast(I32), 0)
-        nc.vector.memset(gs_window[0:GAIN_ROW, 0 : T // 2].bitcast(I32), 0)
-        xs_picked = sb("xs_picked", [P, S], U8)
-        nc.vector.memset(xs_picked[:].bitcast(I32), 0)
+        nc.gpsimd.memset(xs_window[32:64, :].bitcast(I32), 0)
+        nc.gpsimd.memset(xs_window[64:P, :].bitcast(I32), 0)
+        gs_window = placed("gs_window", [P, T], F32, 0)
+        nc.gpsimd.memset(gs_window[0:GAIN_ROW, 0:FILL_POOL].bitcast(I32), 0)
+        nc.vector.memset(gs_window[0:GAIN_ROW, FILL_POOL:FILL_SPLIT].bitcast(I32), 0)
+        xs_planes = [sb("xs_plane%d" % o, [P, S], U8) for o in range(2)]
+        for o in range(2):
+            nc.gpsimd.memset(xs_planes[o][:].bitcast(I32), 0)
+        nc.scalar.activation(
+            gs_window[0:GAIN_ROW, FILL_SPLIT:T], zero[0:GAIN_ROW, :].to_broadcast([GAIN_ROW, T - FILL_SPLIT]), ACT.Gelu_apprx_tanh
+        )
         ident = sb("ident", [P, P], F32)
         make_identity(nc, ident[:])
-        nc.scalar.activation(
-            gs_window[0:GAIN_ROW, T // 2 : T], warm[0:GAIN_ROW, :].to_broadcast([GAIN_ROW, T // 2]), ACT.Gelu_apprx_tanh
-        )
+        w2s_raw = sb("w2s_raw", [P, N], U8)
+        nc.gpsimd.memset(w2s_raw[:].bitcast(I32), 0)
+        for q in range(4):
+            nc.gpsimd.dma_start(
+                w2s_raw[32 * q : 32 * q + 4, :].bitcast(I32), w2_scales[0, 4 * q : 4 * q + 4, :].bitcast(I32)
+            )
 
         w1_rows = w1.rearrange("(o p t) c -> o p t c", p=P, t=PACK)
-        w1_pieces = [(0, 0, H), (1, 0, H)]
-
-        x_window = [placed("x_window0", [P, T], I32, 0), sb("x_window1", [P, T], I32)]
+        w1_raw = [sb("w1_raw%d" % o, [P, PACK, H], F32) for o in range(2)]
+        x_window = [sb("x_window%d" % o, [P, T], I32) for o in range(2)]
 
         def load_x(o, a, b):
             nc.sync.dma_start(x_window[o][:, a:b], x_words[o].rearrange("p n t -> p (n t)").bitcast(I32)[:, a:b])
 
-        def load_w1(n):
-            o, a, b = w1_pieces[n]
-            raw = sb("w1_raw%d" % n, [P, PACK, b - a], F32)
-            nc.sync.dma_start(raw[:], w1_rows[o, :, :, a:b])
-            return raw
-
-        def load_w2_scales(first, last):
-            for q in range(first, last):
+        def move_x_scales(o, rows):
+            for r in rows:
                 nc.sync.dma_start(
-                    w2s_raw[32 * q : 32 * q + 4, :].bitcast(I32), w2_scales[0, 4 * q : 4 * q + 4, :].bitcast(I32)
+                    xs_planes[o][4 * o + r : P : 32, :].bitcast(I32),
+                    xs_gathered[16 * o + r : 16 * o + 16 : 4, :].bitcast(I32),
                 )
 
-        def move_x_scales(first, last):
-            for r, o in [divmod(n, 2) for n in range(first, last)]:
-                nc.sync.dma_start(
-                    xs_picked[4 * o + r : P : 32, :].bitcast(I32),
-                    xs_gathered[64 * o + 4 * r : 64 * o + 64 : 16, :].bitcast(I32),
-                )
-
-        w1_raw = [load_w1(0)]
-        nc.sync.dma_start(xs_window[0:P:4, :].bitcast(I32), x_scales.rearrange("o q c -> (o q) c").bitcast(I32))
-        nc.sync.dma_start(gs_window[GAIN_ROW + 1 : P, :], shift[0:1, :])
+        nc.sync.dma_start(xs_window[0:32, :].bitcast(I32), x_scales.rearrange("o q c -> (o q) c").bitcast(I32))
+        nc.sync.dma_start(gs_window[GAIN_ROW : GAIN_ROW + 1, :], gain[0:1, :])
+        nc.sync.dma_start(gs_window[SHIFT_ROW : SHIFT_ROW + 1, :], shift[0:1, :])
+        nc.sync.dma_start(w1_raw[0][:], w1_rows[0])
+        nc.sync.dma_start(w1_raw[1][:], w1_rows[1])
         wsum_cols = sb("wsum_cols", [P, PACK], F32)
         nc.sync.dma_start(wsum_cols[:], wsum.rearrange("(p t) o -> p (t o)", t=PACK))
-        w2_raw = sb("w2_raw", [P, 2 * N], U8)
-        nc.sync.dma_start(w2_raw[:].bitcast(I32), w2_words[0].bitcast(I32))
-        w1_raw.append(load_w1(1))
-        load_w2_scales(0, 4)
-        load_x(0, 0, T // 2)
+        load_x(0, 0, T)
         xs_gathered = sb("xs_gathered", [P, S], U8)
         nc.vector.tensor_copy(xs_gathered[:], xs_window[:].indirect(offsets[:]))
-        move_x_scales(0, 2)
-        load_x(0, T // 2, T)
-        move_x_scales(2, 8)
-        load_x(1, 0, T)
+        move_x_scales(0, range(4))
+        move_x_scales(1, range(2))
+        load_x(1, 0, X_SPLIT)
+        move_x_scales(1, range(2, 4))
+        load_x(1, X_SPLIT, T)
+        w2_raw = sb("w2_raw", [P, 2 * N], U8)
+        nc.sync.dma_start(w2_raw[:].bitcast(I32), w2_words[0].bitcast(I32))
 
-        gs_picked = sb("gs_picked", [P, S], F32, "xs_window")
+        gs_picked = sb("gs_picked", [P, S], F32)
         nc.vector.tensor_copy(gs_picked[:], gs_window[:].indirect(offsets[:]))
 
-        w1_codes = [sb("w1_codes0", [P, H], U32), placed("w1_codes1", [P, H], U32, 0)]
-        w1_scales = {}
-        w1_grouped = [sb("w1_grouped%d" % n, [P, H, PACK], BF16) for n in range(2)]
-
-        def prepare_w1(n, copy, first, last):
+        w1_grouped = [sb("w1_grouped0", [P, H, PACK], BF16), placed("w1_grouped1", [P, H, PACK], BF16, 0)]
+        w1_codes = [placed("w1_codes%d" % o, [P, H], U32, (4 + 2 * o) * KB) for o in range(2)]
+        w1_scales = [sb("w1_scales%d" % o, [P, H], U8) for o in range(2)]
+        for o, copy in enumerate((nc.scalar.copy, nc.vector.tensor_copy)):
             copy(
-                w1_grouped[n][:].rearrange("p (t m) r -> p m t r", t=PACK)[:, first:last],
-                w1_raw[n][:].rearrange("p r (m t) -> p m t r", t=PACK)[:, first:last],
+                w1_grouped[o][:].rearrange("p (t m) r -> p m t r", t=PACK),
+                w1_raw[o][:].rearrange("p r (m t) -> p m t r", t=PACK),
             )
-
-        def quantize_w1(n):
-            w1_scales[n] = sb("w1_scales%d" % n, [P, H], U8)
             nc.vector.quantize_mx(
-                w1_codes[n][:].bitcast(FP8X4), w1_scales[n][:], w1_grouped[n][:].rearrange("p c r -> p (c r)")
+                w1_codes[o][:].bitcast(FP8X4), w1_scales[o][:], w1_grouped[o][:].rearrange("p c r -> p (c r)")
             )
-
-        prepare_w1(0, nc.scalar.copy, 0, P)
-        quantize_w1(0)
-        prepare_w1(1, nc.scalar.copy, 0, P // 2)
-        prepare_w1(1, nc.vector.tensor_copy, P // 2, P)
 
         wsum_bank = bank(7, "wsum_bank")
         for t in range(PACK):
             nc.tensor.transpose(
                 wsum_bank[:, t * P : (t + 1) * P], wsum_cols[:, t : t + 1].to_broadcast([P, P]), ident[:]
             )
-        wsum_rows = sb("wsum_rows", [P, H], F32, "w1_raw1")
+        wsum_rows = sb("wsum_rows", [P, H], F32)
         nc.scalar.copy(wsum_rows[:], wsum_bank[:])
 
-        gs_cols = sb("gs_cols", [P, TILES, 2], F32)
+        gs_cols = sb("gs_cols", [P, TILES, 2], F32, "w1_raw0")
         for half in range(2):
             gs_bank = bank(5 + half, "gs_bank%d" % half)
             for n in range(4):
@@ -155,7 +134,7 @@ def tile_picked_zdq_mlpgelu_po_kernel(
                 nc.tensor.transpose(gs_bank[:, n * P : (n + 1) * P], gs_picked[:, j * P : (j + 1) * P], ident[:])
             nc.scalar.copy(
                 gs_cols[:, 4 * half : 4 * half + 4, :],
-                gs_bank[:].rearrange("p (n c) -> p n c", n=4)[:, :, GAIN_ROW:P],
+                gs_bank[:].rearrange("p (n c) -> p n c", n=4)[:, :, GAIN_ROW : SHIFT_ROW + 1 : SHIFT_ROW - GAIN_ROW],
             )
 
         offset_term = []
@@ -165,46 +144,34 @@ def tile_picked_zdq_mlpgelu_po_kernel(
                 offset_term[j][:].rearrange("p t m -> p (t m)"), wsum_rows[:], ACT.Copy, scale=gs_cols[:, j, 1:2]
             )
 
-
         y_banks = [bank(j, "y_bank%d" % j) for j in range(TILES)]
         x_picked = {}
 
         def gather_x(o, first, last, tag=None):
-            picked = sb("x_picked%d_%d" % (o, first), [P, (last - first) * P], U32, tag)
+            name, shape = "x_picked%d_%d" % (o, first), [P, (last - first) * P]
+            picked = placed(name, shape, U32, 8 * KB + 4 * P * first) if o == 0 else sb(name, shape, U32, tag)
             nc.vector.tensor_copy(picked[:], x_window[o][:].bitcast(U32).indirect(offsets[:, 8 * first : 8 * last]))
             for j in range(first, last):
                 x_picked[o, j] = picked[:, (j - first) * P : (j - first + 1) * P]
 
-        def first_layer(j, n):
-            o, a, b = w1_pieces[n]
+        def first_layer(j, o):
             nc.tensor.matmul_mx(
-                y_banks[j][:, a:b],
+                y_banks[j][:],
                 lhsT=x_picked[o, j].bitcast(FP8X4),
-                lhsT_scale=xs_picked[4 * o : P, j * P : (j + 1) * P],
-                rhs=w1_codes[n][:].bitcast(FP8X4),
-                rhs_scale=w1_scales[n][:],
-                start=(n == 0),
-                stop=(n == 1),
+                lhsT_scale=xs_planes[o][4 * o : P, j * P : (j + 1) * P],
+                rhs=w1_codes[o][:].bitcast(FP8X4),
+                rhs_scale=w1_scales[o][:],
+                start=(o == 0),
+                stop=(o == 1),
             )
 
-        for half in range(2):
-            gather_x(0, 4 * half, 4 * half + 4)
-            for j in range(4 * half, 4 * half + 4):
-                first_layer(j, 0)
+        for first in range(0, TILES, 2):
+            gather_x(0, first, first + 2)
+            first_layer(first, 0)
+            first_layer(first + 1, 0)
 
-        quantize_w1(1)
-        w2_codes = sb("w2_codes", [P, PACK, 2 * P], U8)
-        nc.vector.tensor_copy(
-            w2_codes[:].rearrange("p t (m b) -> p t m b", b=2), w2_raw[:].rearrange("p (m t b) -> p t m b", t=PACK, b=2)
-        )
-        w2s = placed("w2s", [P, PACK, P], U8, 8 * KB)
-        nc.vector.tensor_copy(w2s[:], w2s_raw[:].rearrange("p (m t) -> p t m", t=PACK))
-
-        for first in (0, 2):
-            gather_x(1, first, first + 2)
-            first_layer(first, 1)
-            first_layer(first + 1, 1)
-        gather_x(1, 4, 6)
+        w2s = sb("w2s", [P, PACK, P], U8)
+        nc.gpsimd.tensor_copy(w2s[:], w2s_raw[:].rearrange("p (m t) -> p t m", t=PACK))
 
         out_codes = sb("out_codes", [P, S], I32)
         out_scales = sb("out_scales", [P, S], U8)
@@ -214,24 +181,24 @@ def tile_picked_zdq_mlpgelu_po_kernel(
         unit_of = {j: u for u, (a, b) in enumerate(units) for j in range(a, b)}
         h_grouped = [sb("h_grouped%d" % u, [P, (b - a) * P, PACK], BF16) for u, (a, b) in enumerate(units)]
         result = [sb("result%d" % u, [P, PACK, (b - a) * P], F32) for u, (a, b) in enumerate(units)]
-        out_banks = {}
-        pre = {}
-        on_scalar = (0,)
+        out_grouped = [sb("out_grouped%d" % u, [P, (b - a) * P, PACK], BF16) for u, (a, b) in enumerate(units)]
+        h_codes, h_scales, out_banks, pre = {}, {}, {}, {}
 
         def scale(j):
-            pre[j] = sb("pre%d" % j, [P, PACK, P], F32)
-            y_dealt = y_banks[j][:].rearrange("p (t m) -> p t m", t=PACK)
-            if j in on_scalar:
-                nc.scalar.activation(pre[j][:], y_dealt, ACT.Copy, scale=gs_cols[:, j, 0:1])
+            pre[j] = sb("pre%d" % j, [P, H], F32)
+            if j == 0:
+                nc.scalar.activation(pre[j][:], y_banks[j][:], ACT.Copy, scale=gs_cols[:, j, 0:1])
             else:
-                nc.vector.scalar_tensor_tensor(pre[j][:], y_dealt, gs_cols[:, j, 0:1], offset_term[j][:], MULT, ADD)
+                nc.vector.scalar_tensor_tensor(
+                    pre[j][:], y_banks[j][:], gs_cols[:, j, 0:1], offset_term[j][:].rearrange("p t m -> p (t m)"), MULT, ADD
+                )
 
         def hidden(j):
             turned = bank(j, "turned%d" % j)
             for t in range(PACK):
                 out = turned[:, t * P : (t + 1) * P]
-                nc.tensor.matmul(out, pre[j][:, t, :], ident[:], start=True, stop=j not in on_scalar, is_transpose=True)
-                if j in on_scalar:
+                nc.tensor.matmul(out, pre[j][:, t * P : (t + 1) * P], ident[:], start=True, stop=j != 0, is_transpose=True)
+                if j == 0:
                     nc.tensor.matmul(out, offset_term[j][:, t, :], ident[:], start=False, stop=True, is_transpose=True)
             place = j - units[unit_of[j]][0]
             nc.scalar.activation(
@@ -240,38 +207,42 @@ def tile_picked_zdq_mlpgelu_po_kernel(
                 ACT.Gelu_apprx_tanh,
             )
 
+        def quantize_h(u):
+            a, b = units[u]
+            h_codes[u] = sb("h_codes%d" % u, [P, (b - a) * P], U32)
+            h_scales[u] = sb("h_scales%d" % u, [P, (b - a) * P], U8)
+            nc.vector.quantize_mx(
+                h_codes[u][:].bitcast(FP8X4), h_scales[u][:], h_grouped[u][:].rearrange("p j t -> p (j t)")
+            )
+
         def second_layer(u):
             a, b = units[u]
             width = (b - a) * P
-            h_codes = sb("h_codes%d" % u, [P, width], U32)
-            h_scales = sb("h_scales%d" % u, [P, width], U8)
-            nc.vector.quantize_mx(h_codes[:].bitcast(FP8X4), h_scales[:], h_grouped[u][:].rearrange("p j t -> p (j t)"))
             out_banks[u] = [bank(j, "out_bank%d" % j) for j in range(a, b)]
             for t in range(PACK):
                 n, place = divmod(t * width, 512)
                 nc.tensor.matmul_mx(
                     out_banks[u][n][:, place : place + width],
-                    lhsT=w2_codes[:, t, :].bitcast(FP4X4),
+                    lhsT=w2_codes[:, t, :].bitcast(U8).bitcast(FP4X4),
                     lhsT_scale=w2s[:, t, :],
-                    rhs=h_codes[:].bitcast(FP8X4),
-                    rhs_scale=h_scales[:],
+                    rhs=h_codes[u][:].bitcast(FP8X4),
+                    rhs_scale=h_scales[u][:],
                     start=True,
                     stop=True,
                 )
 
-        def leave(u, copies):
+        def leave(u, n, copy):
             a, b = units[u]
             rows = PACK // (b - a)
-            for n in range(b - a):
-                part = result[u][:, rows * n : rows * (n + 1), :]
-                copies[n](part.rearrange("p t j -> p (t j)"), out_banks[u][n][:])
-                nc.sync.dma_start(out_rows[:, rows * n : rows * (n + 1), a * P : b * P], part)
-
-        out_grouped = [sb("out_grouped%d" % u, [P, (b - a) * P, PACK], BF16) for u, (a, b) in enumerate(units)]
+            part = result[u][:, rows * n : rows * (n + 1), :]
+            copy(part.rearrange("p t j -> p (t j)"), out_banks[u][n][:])
+            nc.sync.dma_start(out_rows[:, rows * n : rows * (n + 1), a * P : b * P], part)
 
         def round_result(u):
-            dst, src = interleave_views(out_grouped[u][:], result[u][:])
-            nc.vector.tensor_copy(dst, src)
+            nc.vector.tensor_copy(
+                out_grouped[u][:].rearrange("p (c i) t -> p c t i", i=4),
+                result[u][:].rearrange("p t (c i) -> p c t i", i=4),
+            )
 
         def planes(u):
             a, b = units[u]
@@ -284,42 +255,59 @@ def tile_picked_zdq_mlpgelu_po_kernel(
                 nc.sync.dma_start(out_words[:, cols], out_codes[:, cols])
 
         V, A = nc.vector.tensor_copy, nc.scalar.copy
-        first_layer(4, 1)
-        first_layer(5, 1)
+        for first in (0, 2, 4):
+            gather_x(1, first, first + 2)
+            first_layer(first, 1)
+            first_layer(first + 1, 1)
         scale(0)
+        w2_codes = sb("w2_codes", [P, PACK, P], U16, "x_picked1_0")
+        nc.scalar.copy(w2_codes[:], w2_raw[:].bitcast(U16).rearrange("p (m t) -> p t m", t=PACK))
         scale(1)
-        gather_x(1, 6, 8, "offset_term1")
         scale(2)
-        scale(3)
+        gather_x(1, 6, 8, "offset_term1")
         hidden(0)
         hidden(1)
-        first_layer(6, 1)
-        scale(4)
-        scale(5)
         hidden(2)
-        hidden(3)
+        first_layer(6, 1)
         first_layer(7, 1)
-        scale(6)
-        second_layer(0)
-        scale(7)
-        leave(0, (A, V))
+        scale(3)
+        hidden(3)
+        scale(4)
         hidden(4)
+        scale(5)
         hidden(5)
-        second_layer(1)
+        quantize_h(0)
+        second_layer(0)
+        scale(6)
+        scale(7)
+        leave(0, 0, A)
         hidden(6)
         hidden(7)
+        quantize_h(1)
+        second_layer(1)
+        leave(0, 1, V)
+        quantize_h(2)
         second_layer(2)
-        second_layer(3)
-        second_layer(4)
-        leave(1, (V, A))
-        leave(2, (A, A))
-        leave(3, (A,))
-        leave(4, (A,))
         round_result(0)
-        for u in range(1, len(units)):
-            round_result(u)
-            planes(u - 1)
-        planes(len(units) - 1)
+        quantize_h(3)
+        second_layer(3)
+        planes(0)
+        quantize_h(4)
+        second_layer(4)
+        leave(1, 0, A)
+        leave(1, 1, A)
+        round_result(1)
+        leave(2, 0, A)
+        leave(2, 1, A)
+        planes(1)
+        round_result(2)
+        leave(3, 0, A)
+        round_result(3)
+        planes(2)
+        leave(4, 0, A)
+        round_result(4)
+        planes(3)
+        planes(4)
         for q in range(4):
             engine = nc.sync if q < 2 else nc.scalar
             engine.dma_start(

@@ -21,10 +21,9 @@ ADD = mybir.AluOpType.add
 P = 128
 PACK = 4
 TILES = S // P
-GAIN_ROW, SHIFT_ROW = 126, 127
-FILL_POOL, FILL_SPLIT = 1088, 3339
-X_SPLIT = 3 * T // 4
-KB = 1024
+GAIN_ROW, SHIFT_ROW = 63, 127
+FILL_SPLIT = 2304
+X_EARLY, X_SPLIT = T // 8, 3 * T // 4
 
 
 def tile_picked_zdq_mlpgelu_po_kernel(
@@ -33,14 +32,10 @@ def tile_picked_zdq_mlpgelu_po_kernel(
     nc = tc.nc
     with ExitStack() as ctx:
         keep = ctx.enter_context(tc.tile_pool(name="keep", bufs=1))
-        reuse = ctx.enter_context(tc.tile_pool(name="reuse", bufs=1))
         psum = ctx.enter_context(tc.psum_pool(name="psum", bufs=1))
 
         def sb(name, shape, dtype, tag=None):
             return keep.tile(shape, dtype, name=name, tag=tag or name, align_bytes=64)
-
-        def placed(name, shape, dtype, offset):
-            return reuse.tile(shape, dtype, name=name, align_bytes=64, offset=offset)
 
         def bank(index, name):
             return psum.tile([P, 512], F32, name=name, tag="bank%d" % index)
@@ -48,28 +43,22 @@ def tile_picked_zdq_mlpgelu_po_kernel(
         offsets = keep.tile([P, S // 16], U16, name="offsets")
         nc.sync.dma_start(offsets[:], offs)
 
+        xs_window = sb("xs_window", [P, T], U8)
+        nc.vector.memset(xs_window[:].bitcast(I32), 0)
+        w2s_raw = sb("w2s_raw", [P, N], U8)
+        nc.gpsimd.memset(w2s_raw[:].bitcast(I32), 0)
         zero = sb("zero", [P, 1], F32)
         nc.vector.memset(zero[:], 0.0)
-        xs_window = sb("xs_window", [P, T], U8)
-        nc.gpsimd.memset(xs_window[32:64, :].bitcast(I32), 0)
-        nc.gpsimd.memset(xs_window[64:P, :].bitcast(I32), 0)
-        gs_window = placed("gs_window", [P, T], F32, 0)
-        nc.gpsimd.memset(gs_window[0:GAIN_ROW, 0:FILL_POOL].bitcast(I32), 0)
-        nc.vector.memset(gs_window[0:GAIN_ROW, FILL_POOL:FILL_SPLIT].bitcast(I32), 0)
+        gs_window = sb("gs_window", [P, T], F32)
+        nc.vector.memset(gs_window[:, 0:FILL_SPLIT].bitcast(I32), 0)
+        nc.scalar.activation(
+            gs_window[:, FILL_SPLIT:T], zero[:].to_broadcast([P, T - FILL_SPLIT]), ACT.Gelu_apprx_tanh
+        )
         xs_planes = [sb("xs_plane%d" % o, [P, S], U8) for o in range(2)]
         for o in range(2):
             nc.gpsimd.memset(xs_planes[o][:].bitcast(I32), 0)
-        nc.scalar.activation(
-            gs_window[0:GAIN_ROW, FILL_SPLIT:T], zero[0:GAIN_ROW, :].to_broadcast([GAIN_ROW, T - FILL_SPLIT]), ACT.Gelu_apprx_tanh
-        )
         ident = sb("ident", [P, P], F32)
         make_identity(nc, ident[:])
-        w2s_raw = sb("w2s_raw", [P, N], U8)
-        nc.gpsimd.memset(w2s_raw[:].bitcast(I32), 0)
-        for q in range(4):
-            nc.gpsimd.dma_start(
-                w2s_raw[32 * q : 32 * q + 4, :].bitcast(I32), w2_scales[0, 4 * q : 4 * q + 4, :].bitcast(I32)
-            )
 
         w1_rows = w1.rearrange("(o p t) c -> o p t c", p=P, t=PACK)
         w1_raw = [sb("w1_raw%d" % o, [P, PACK, H], F32) for o in range(2)]
@@ -82,32 +71,35 @@ def tile_picked_zdq_mlpgelu_po_kernel(
             for r in rows:
                 nc.sync.dma_start(
                     xs_planes[o][4 * o + r : P : 32, :].bitcast(I32),
-                    xs_gathered[16 * o + r : 16 * o + 16 : 4, :].bitcast(I32),
+                    xs_gathered[64 * o + 4 * r : 64 * o + 64 : 16, :].bitcast(I32),
                 )
 
-        nc.sync.dma_start(xs_window[0:32, :].bitcast(I32), x_scales.rearrange("o q c -> (o q) c").bitcast(I32))
-        nc.sync.dma_start(gs_window[GAIN_ROW : GAIN_ROW + 1, :], gain[0:1, :])
-        nc.sync.dma_start(gs_window[SHIFT_ROW : SHIFT_ROW + 1, :], shift[0:1, :])
         nc.sync.dma_start(w1_raw[0][:], w1_rows[0])
+        nc.sync.dma_start(xs_window[0:P:4, :].bitcast(I32), x_scales.rearrange("o q c -> (o q) c").bitcast(I32))
+        for q in range(4):
+            nc.sync.dma_start(
+                w2s_raw[32 * q : 32 * q + 4, :].bitcast(I32), w2_scales[0, 4 * q : 4 * q + 4, :].bitcast(I32)
+            )
         nc.sync.dma_start(w1_raw[1][:], w1_rows[1])
         wsum_cols = sb("wsum_cols", [P, PACK], F32)
         nc.sync.dma_start(wsum_cols[:], wsum.rearrange("(p t) o -> p (t o)", t=PACK))
+        nc.sync.dma_start(gs_window[GAIN_ROW : GAIN_ROW + 1, :], gain[0:1, :])
+        nc.sync.dma_start(gs_window[SHIFT_ROW : SHIFT_ROW + 1, :], shift[0:1, :])
+        load_x(1, 0, X_EARLY)
         load_x(0, 0, T)
         xs_gathered = sb("xs_gathered", [P, S], U8)
         nc.vector.tensor_copy(xs_gathered[:], xs_window[:].indirect(offsets[:]))
         move_x_scales(0, range(4))
         move_x_scales(1, range(2))
-        load_x(1, 0, X_SPLIT)
+        load_x(1, X_EARLY, X_SPLIT)
         move_x_scales(1, range(2, 4))
         load_x(1, X_SPLIT, T)
         w2_raw = sb("w2_raw", [P, 2 * N], U8)
         nc.sync.dma_start(w2_raw[:].bitcast(I32), w2_words[0].bitcast(I32))
 
-        gs_picked = sb("gs_picked", [P, S], F32)
-        nc.vector.tensor_copy(gs_picked[:], gs_window[:].indirect(offsets[:]))
 
-        w1_grouped = [sb("w1_grouped0", [P, H, PACK], BF16), placed("w1_grouped1", [P, H, PACK], BF16, 0)]
-        w1_codes = [placed("w1_codes%d" % o, [P, H], U32, (4 + 2 * o) * KB) for o in range(2)]
+        w1_grouped = [sb("w1_grouped%d" % o, [P, H, PACK], BF16) for o in range(2)]
+        w1_codes = [sb("w1_codes%d" % o, [P, H], U32) for o in range(2)]
         w1_scales = [sb("w1_scales%d" % o, [P, H], U8) for o in range(2)]
         for o, copy in enumerate((nc.scalar.copy, nc.vector.tensor_copy)):
             copy(
@@ -126,30 +118,34 @@ def tile_picked_zdq_mlpgelu_po_kernel(
         wsum_rows = sb("wsum_rows", [P, H], F32)
         nc.scalar.copy(wsum_rows[:], wsum_bank[:])
 
-        gs_cols = sb("gs_cols", [P, TILES, 2], F32, "w1_raw0")
+        gs_cols = sb("gs_cols", [P, TILES, 2], F32)
         for half in range(2):
+            gs_picked = sb("gs_picked%d" % half, [P, S // 2], F32)
+            nc.scalar.activation(gs_picked[:], gs_window[:].indirect(offsets[:, 32 * half : 32 * half + 32]), ACT.Copy)
             gs_bank = bank(5 + half, "gs_bank%d" % half)
             for n in range(4):
-                j = 4 * half + n
-                nc.tensor.transpose(gs_bank[:, n * P : (n + 1) * P], gs_picked[:, j * P : (j + 1) * P], ident[:])
+                nc.tensor.transpose(gs_bank[:, n * P : (n + 1) * P], gs_picked[:, n * P : (n + 1) * P], ident[:])
             nc.scalar.copy(
                 gs_cols[:, 4 * half : 4 * half + 4, :],
                 gs_bank[:].rearrange("p (n c) -> p n c", n=4)[:, :, GAIN_ROW : SHIFT_ROW + 1 : SHIFT_ROW - GAIN_ROW],
             )
 
-        offset_term = []
-        for j in range(TILES):
-            offset_term.append(sb("offset_term%d" % j, [P, PACK, P], F32))
+        offset_term = {}
+
+        def make_offset_term(j, tag=None):
+            offset_term[j] = sb("offset_term%d" % j, [P, PACK, P], F32, tag)
             nc.scalar.activation(
                 offset_term[j][:].rearrange("p t m -> p (t m)"), wsum_rows[:], ACT.Copy, scale=gs_cols[:, j, 1:2]
             )
+
+        for j in range(TILES - 2):
+            make_offset_term(j)
 
         y_banks = [bank(j, "y_bank%d" % j) for j in range(TILES)]
         x_picked = {}
 
         def gather_x(o, first, last, tag=None):
-            name, shape = "x_picked%d_%d" % (o, first), [P, (last - first) * P]
-            picked = placed(name, shape, U32, 8 * KB + 4 * P * first) if o == 0 else sb(name, shape, U32, tag)
+            picked = sb("x_picked%d_%d" % (o, first), [P, (last - first) * P], U32, tag)
             nc.vector.tensor_copy(picked[:], x_window[o][:].bitcast(U32).indirect(offsets[:, 8 * first : 8 * last]))
             for j in range(first, last):
                 x_picked[o, j] = picked[:, (j - first) * P : (j - first + 1) * P]
@@ -170,8 +166,8 @@ def tile_picked_zdq_mlpgelu_po_kernel(
             first_layer(first, 0)
             first_layer(first + 1, 0)
 
-        w2s = sb("w2s", [P, PACK, P], U8)
-        nc.gpsimd.tensor_copy(w2s[:], w2s_raw[:].rearrange("p (m t) -> p t m", t=PACK))
+        w2s = sb("w2s", [P, PACK, P], U8, "w1_grouped0")
+        nc.vector.tensor_copy(w2s[:], w2s_raw[:].rearrange("p (m t) -> p t m", t=PACK))
 
         out_codes = sb("out_codes", [P, S], I32)
         out_scales = sb("out_scales", [P, S], U8)
@@ -262,6 +258,8 @@ def tile_picked_zdq_mlpgelu_po_kernel(
         scale(0)
         w2_codes = sb("w2_codes", [P, PACK, P], U16, "x_picked1_0")
         nc.scalar.copy(w2_codes[:], w2_raw[:].bitcast(U16).rearrange("p (m t) -> p t m", t=PACK))
+        make_offset_term(6, "x_picked1_2")
+        make_offset_term(7, "x_picked1_4")
         scale(1)
         scale(2)
         gather_x(1, 6, 8, "offset_term1")
@@ -274,29 +272,29 @@ def tile_picked_zdq_mlpgelu_po_kernel(
         hidden(3)
         scale(4)
         hidden(4)
-        scale(5)
-        hidden(5)
         quantize_h(0)
         second_layer(0)
+        scale(5)
         scale(6)
-        scale(7)
-        leave(0, 0, A)
-        hidden(6)
-        hidden(7)
+        leave(0, 1, A)
+        hidden(5)
+        leave(0, 0, V)
         quantize_h(1)
+        hidden(6)
         second_layer(1)
-        leave(0, 1, V)
+        scale(7)
+        leave(1, 0, A)
+        hidden(7)
+        round_result(0)
         quantize_h(2)
         second_layer(2)
-        round_result(0)
+        leave(1, 1, V)
+        planes(0)
         quantize_h(3)
         second_layer(3)
-        planes(0)
+        round_result(1)
         quantize_h(4)
         second_layer(4)
-        leave(1, 0, A)
-        leave(1, 1, A)
-        round_result(1)
         leave(2, 0, A)
         leave(2, 1, A)
         planes(1)

@@ -23,7 +23,7 @@ PACK = 4
 TILES = S // P
 GAIN_ROW, SHIFT_ROW = 63, 127
 FILL_SPLIT = 2304
-X_EARLY, X_SPLIT = T // 8, 3 * T // 4
+X_EARLY = T // 8
 
 
 def tile_picked_zdq_mlpgelu_po_kernel(
@@ -76,10 +76,7 @@ def tile_picked_zdq_mlpgelu_po_kernel(
 
         nc.sync.dma_start(w1_raw[0][:], w1_rows[0])
         nc.sync.dma_start(xs_window[0:P:4, :].bitcast(I32), x_scales.rearrange("o q c -> (o q) c").bitcast(I32))
-        for q in range(4):
-            nc.sync.dma_start(
-                w2s_raw[32 * q : 32 * q + 4, :].bitcast(I32), w2_scales[0, 4 * q : 4 * q + 4, :].bitcast(I32)
-            )
+        nc.sync.dma_start(w2s_raw[0:P:8, :].bitcast(I32), w2_scales[0].bitcast(I32))
         nc.sync.dma_start(w1_raw[1][:], w1_rows[1])
         wsum_cols = sb("wsum_cols", [P, PACK], F32)
         nc.sync.dma_start(wsum_cols[:], wsum.rearrange("(p t) o -> p (t o)", t=PACK))
@@ -90,10 +87,8 @@ def tile_picked_zdq_mlpgelu_po_kernel(
         xs_gathered = sb("xs_gathered", [P, S], U8)
         nc.vector.tensor_copy(xs_gathered[:], xs_window[:].indirect(offsets[:]))
         move_x_scales(0, range(4))
-        move_x_scales(1, range(2))
-        load_x(1, X_EARLY, X_SPLIT)
-        move_x_scales(1, range(2, 4))
-        load_x(1, X_SPLIT, T)
+        load_x(1, X_EARLY, T)
+        move_x_scales(1, range(4))
         w2_raw = sb("w2_raw", [P, 2 * N], U8)
         nc.sync.dma_start(w2_raw[:].bitcast(I32), w2_words[0].bitcast(I32))
 
@@ -168,6 +163,9 @@ def tile_picked_zdq_mlpgelu_po_kernel(
 
         w2s = sb("w2s", [P, PACK, P], U8, "w1_grouped0")
         nc.vector.tensor_copy(w2s[:], w2s_raw[:].rearrange("p (m t) -> p t m", t=PACK))
+        w2s_rows = w2s[:].rearrange("p t m -> p (t m)").bitcast(I32)
+        for r in range(1, 4):
+            nc.sync.dma_start(w2s_rows[r:P:32, :], w2s_rows[8 * r : P : 32, :])
 
         out_codes = sb("out_codes", [P, S], I32)
         out_scales = sb("out_scales", [P, S], U8)

@@ -172,9 +172,10 @@ def tile_picked_zdq_mlpgelu_po_kernel(
         out_rows = out_0.rearrange("(p t) j -> p t j", t=PACK)
         out_words = out_1[0].rearrange("p j r -> p (j r)").bitcast(I32)
         units = [(0, 2), (2, 4), (4, 6), (6, 7), (7, 8)]
+        word_stores = {4: 0, 6: 4, 8: 6}
         unit_of = {j: u for u, (a, b) in enumerate(units) for j in range(a, b)}
         h_grouped = [sb("h_grouped%d" % u, [P, (b - a) * P, PACK], BF16) for u, (a, b) in enumerate(units)]
-        result = [sb("result%d" % u, [P, PACK, (b - a) * P], F32) for u, (a, b) in enumerate(units)]
+        result = [sb("result%d" % n, [P, PACK, 2 * P], F32) for n in range(TILES // 2)]
         out_grouped = [sb("out_grouped%d" % u, [P, (b - a) * P, PACK], BF16) for u, (a, b) in enumerate(units)]
         h_codes, h_scales, out_banks, pre = {}, {}, {}, {}
 
@@ -228,14 +229,19 @@ def tile_picked_zdq_mlpgelu_po_kernel(
         def leave(u, n, copy):
             a, b = units[u]
             rows = PACK // (b - a)
-            part = result[u][:, rows * n : rows * (n + 1), :]
-            copy(part.rearrange("p t j -> p (t j)"), out_banks[u][n][:])
-            nc.sync.dma_start(out_rows[:, rows * n : rows * (n + 1), a * P : b * P], part)
+            part = result[a // 2][:, rows * n : rows * (n + 1), a % 2 * P : (a % 2 + b - a) * P]
+            copy(part, out_banks[u][n][:].rearrange("p (t j) -> p t j", t=rows))
+            if b % 2 == 0:
+                nc.sync.dma_start(
+                    out_rows[:, rows * n : rows * (n + 1), (b - 2) * P : b * P],
+                    result[a // 2][:, rows * n : rows * (n + 1), :],
+                )
 
         def round_result(u):
+            a, b = units[u]
             nc.vector.tensor_copy(
                 out_grouped[u][:].rearrange("p (c i) t -> p c t i", i=4),
-                result[u][:].rearrange("p t (c i) -> p c t i", i=4),
+                result[a // 2][:, :, a % 2 * P : (a % 2 + b - a) * P].rearrange("p t (c i) -> p c t i", i=4),
             )
 
         def planes(u):
@@ -244,8 +250,8 @@ def tile_picked_zdq_mlpgelu_po_kernel(
             nc.vector.quantize_mx(
                 out_codes[:, cols].bitcast(FP8X4), out_scales[:, cols], out_grouped[u][:].rearrange("p j t -> p (j t)")
             )
-            if b % 2 == 0:
-                cols = slice((b - 2) * P, b * P)
+            if b in word_stores:
+                cols = slice(word_stores[b] * P, b * P)
                 nc.sync.dma_start(out_words[:, cols], out_codes[:, cols])
 
         V, A = nc.vector.tensor_copy, nc.scalar.copy
@@ -276,31 +282,31 @@ def tile_picked_zdq_mlpgelu_po_kernel(
         scale(6)
         leave(0, 1, A)
         hidden(5)
-        leave(0, 0, V)
         quantize_h(1)
         hidden(6)
         second_layer(1)
+        leave(0, 0, V)
         scale(7)
         leave(1, 0, A)
-        hidden(7)
-        round_result(0)
         quantize_h(2)
-        second_layer(2)
         leave(1, 1, V)
-        planes(0)
+        hidden(7)
+        second_layer(2)
+        round_result(0)
         quantize_h(3)
         second_layer(3)
-        round_result(1)
+        planes(0)
         quantize_h(4)
         second_layer(4)
         leave(2, 0, A)
         leave(2, 1, A)
+        round_result(1)
         planes(1)
-        round_result(2)
         leave(3, 0, A)
+        round_result(2)
+        leave(4, 0, A)
         round_result(3)
         planes(2)
-        leave(4, 0, A)
         round_result(4)
         planes(3)
         planes(4)

@@ -41,7 +41,6 @@ def tile_picked_zdq_mlpgelu_po_kernel(
             return psum.tile([P, 512], F32, name=name, tag="bank%d" % index)
 
         offsets = keep.tile([P, S // 16], U16, name="offsets")
-        nc.sync.dma_start(offsets[:], offs)
 
         xs_window = sb("xs_window", [P, T], U8)
         nc.vector.memset(xs_window[:].bitcast(I32), 0)
@@ -75,6 +74,7 @@ def tile_picked_zdq_mlpgelu_po_kernel(
                 )
 
         nc.sync.dma_start(w1_raw[0][:], w1_rows[0])
+        nc.sync.dma_start(offsets[:], offs)
         nc.sync.dma_start(xs_window[0:P:4, :].bitcast(I32), x_scales.rearrange("o q c -> (o q) c").bitcast(I32))
         nc.sync.dma_start(w2s_raw[0:P:8, :].bitcast(I32), w2_scales[0].bitcast(I32))
         nc.sync.dma_start(w1_raw[1][:], w1_rows[1])
@@ -172,7 +172,7 @@ def tile_picked_zdq_mlpgelu_po_kernel(
         out_rows = out_0.rearrange("(p t) j -> p t j", t=PACK)
         out_words = out_1[0].rearrange("p j r -> p (j r)").bitcast(I32)
         units = [(0, 2), (2, 4), (4, 6), (6, 7), (7, 8)]
-        word_stores = {4: 0, 6: 4, 8: 6}
+        word_stores = {2: 0, 4: 2, 6: 4, 8: 6}
         unit_of = {j: u for u, (a, b) in enumerate(units) for j in range(a, b)}
         h_grouped = [sb("h_grouped%d" % u, [P, (b - a) * P, PACK], BF16) for u, (a, b) in enumerate(units)]
         result = [sb("result%d" % n, [P, PACK, 2 * P], F32) for n in range(TILES // 2)]
@@ -180,7 +180,7 @@ def tile_picked_zdq_mlpgelu_po_kernel(
         h_codes, h_scales, out_banks, pre = {}, {}, {}, {}
 
         def scale(j):
-            pre[j] = sb("pre%d" % j, [P, H], F32)
+            pre[j] = sb("pre%d" % j, [P, H], F32, {6: "h_grouped0", 7: "h_grouped1"}.get(j))
             if j == 0:
                 nc.scalar.activation(pre[j][:], y_banks[j][:], ACT.Copy, scale=gs_cols[:, j, 0:1])
             else:
@@ -276,12 +276,12 @@ def tile_picked_zdq_mlpgelu_po_kernel(
         hidden(3)
         scale(4)
         hidden(4)
+        scale(5)
         quantize_h(0)
         second_layer(0)
-        scale(5)
+        hidden(5)
         scale(6)
         leave(0, 1, A)
-        hidden(5)
         quantize_h(1)
         hidden(6)
         second_layer(1)
@@ -301,13 +301,13 @@ def tile_picked_zdq_mlpgelu_po_kernel(
         leave(2, 0, A)
         leave(2, 1, A)
         round_result(1)
-        planes(1)
         leave(3, 0, A)
         round_result(2)
+        planes(1)
         leave(4, 0, A)
+        nc.scalar.copy(out_grouped[4][:], out_banks[4][0][:].rearrange("p (t j) -> p j t", t=PACK))
         round_result(3)
         planes(2)
-        round_result(4)
         planes(3)
         planes(4)
         for q in range(4):

@@ -180,7 +180,7 @@ def tile_picked_zdq_mlpgelu_po_kernel(
         h_codes, h_scales, out_banks, pre = {}, {}, {}, {}
 
         def scale(j):
-            pre[j] = sb("pre%d" % j, [P, H], F32, {6: "h_grouped0", 7: "h_grouped1"}.get(j))
+            pre[j] = sb("pre%d" % j, [P, H], F32, {6: "h_grouped0", 7: "h_codes0"}.get(j))
             if j == 0:
                 nc.scalar.activation(pre[j][:], y_banks[j][:], ACT.Copy, scale=gs_cols[:, j, 0:1])
             else:
@@ -277,18 +277,18 @@ def tile_picked_zdq_mlpgelu_po_kernel(
         scale(4)
         hidden(4)
         scale(5)
+        hidden(5)
         quantize_h(0)
         second_layer(0)
-        hidden(5)
         scale(6)
-        leave(0, 1, A)
         quantize_h(1)
+        leave(0, 0, V)
+        leave(0, 1, A)
         hidden(6)
         second_layer(1)
-        leave(0, 0, V)
         scale(7)
-        leave(1, 0, A)
         quantize_h(2)
+        leave(1, 0, A)
         leave(1, 1, V)
         hidden(7)
         second_layer(2)

@@ -21,7 +21,7 @@ ADD = mybir.AluOpType.add
 P = 128
 PACK = 4
 TILES = S // P
-GAIN_ROW, SHIFT_ROW = 63, 127
+FIRST_ROW, ROW_STEP = 19, 36
 FILL_SPLIT = 2304
 X_EARLY = T // 8
 
@@ -80,8 +80,9 @@ def tile_picked_zdq_mlpgelu_po_kernel(
         nc.sync.dma_start(w1_raw[1][:], w1_rows[1])
         wsum_cols = sb("wsum_cols", [P, PACK], F32)
         nc.sync.dma_start(wsum_cols[:], wsum.rearrange("(p t) o -> p (t o)", t=PACK))
-        nc.sync.dma_start(gs_window[GAIN_ROW : GAIN_ROW + 1, :], gain[0:1, :])
-        nc.sync.dma_start(gs_window[SHIFT_ROW : SHIFT_ROW + 1, :], shift[0:1, :])
+        for n, (half, table) in enumerate(((0, gain), (0, shift), (1, gain), (1, shift))):
+            row, cols = FIRST_ROW + n * ROW_STEP, slice(half * T // 2, (half + 1) * T // 2)
+            nc.sync.dma_start(gs_window[row : row + 1, cols], table[0:1, cols])
         load_x(1, 0, X_EARLY)
         load_x(0, 0, T)
         xs_gathered = sb("xs_gathered", [P, S], U8)
@@ -120,10 +121,9 @@ def tile_picked_zdq_mlpgelu_po_kernel(
             gs_bank = bank(5 + half, "gs_bank%d" % half)
             for n in range(4):
                 nc.tensor.transpose(gs_bank[:, n * P : (n + 1) * P], gs_picked[:, n * P : (n + 1) * P], ident[:])
-            nc.scalar.copy(
-                gs_cols[:, 4 * half : 4 * half + 4, :],
-                gs_bank[:].rearrange("p (n c) -> p n c", n=4)[:, :, GAIN_ROW : SHIFT_ROW + 1 : SHIFT_ROW - GAIN_ROW],
-            )
+            gs_parts = sb("gs_parts%d" % half, [P, 4, 4], F32)
+            nc.scalar.copy(gs_parts[:], gs_bank[:].rearrange("p (n c) -> p n c", n=4)[:, :, FIRST_ROW:P:ROW_STEP])
+            nc.gpsimd.tensor_tensor(gs_cols[:, 4 * half : 4 * half + 4, :], gs_parts[:, :, 0:2], gs_parts[:, :, 2:4], ADD)
 
         offset_term = {}
 
@@ -133,7 +133,7 @@ def tile_picked_zdq_mlpgelu_po_kernel(
                 offset_term[j][:].rearrange("p t m -> p (t m)"), wsum_rows[:], ACT.Copy, scale=gs_cols[:, j, 1:2]
             )
 
-        for j in range(TILES - 2):
+        for j in range(TILES - 1):
             make_offset_term(j)
 
         y_banks = [bank(j, "y_bank%d" % j) for j in range(TILES)]
@@ -262,8 +262,7 @@ def tile_picked_zdq_mlpgelu_po_kernel(
         scale(0)
         w2_codes = sb("w2_codes", [P, PACK, P], U16, "x_picked1_0")
         nc.scalar.copy(w2_codes[:], w2_raw[:].bitcast(U16).rearrange("p (m t) -> p t m", t=PACK))
-        make_offset_term(6, "x_picked1_2")
-        make_offset_term(7, "x_picked1_4")
+        make_offset_term(7, "x_picked1_2")
         scale(1)
         scale(2)
         gather_x(1, 6, 8, "offset_term1")

from contextlib import ExitStack

import concourse.mybir as mybir
from concourse.masks import make_identity

K, T, S, H, N = 1024, 4096, 1024, 512, 512
FLOPS = 2 * K * H * S + 2 * H * N * S

F32 = mybir.dt.float32
BF16 = mybir.dt.bfloat16
I32 = mybir.dt.int32
U32 = mybir.dt.uint32
U16 = mybir.dt.uint16
U8 = mybir.dt.uint8
FP8X4 = mybir.dt.float8_e4m3fn_x4
FP4X4 = mybir.dt.float4_e2m1fn_x4
ACT = mybir.ActivationFunctionType
MULT = mybir.AluOpType.mult
ADD = mybir.AluOpType.add

P = 128
PACK = 4
TILES = S // P
FIRST_ROW, ROW_STEP = 19, 36
FILL_SPLIT = 2304
X_EARLY = T // 8


def tile_picked_zdq_mlpgelu_po_kernel(
    tc, x_words, x_scales, w1, gain, shift, wsum, w2_words, w2_scales, offs, out_0, out_1, out_2
):
    nc = tc.nc
    with ExitStack() as ctx:
        keep = ctx.enter_context(tc.tile_pool(name="keep", bufs=1))
        psum = ctx.enter_context(tc.psum_pool(name="psum", bufs=1))

        def sb(name, shape, dtype, tag=None):
            return keep.tile(shape, dtype, name=name, tag=tag or name, align_bytes=64)

        def bank(index, name):
            return psum.tile([P, 512], F32, name=name, tag="bank%d" % index)

        offsets = keep.tile([P, S // 16], U16, name="offsets")

        xs_window = sb("xs_window", [P, T], U8)
        nc.vector.memset(xs_window[:].bitcast(I32), 0)
        w2s_raw = sb("w2s_raw", [P, N], U8)
        nc.gpsimd.memset(w2s_raw[:].bitcast(I32), 0)
        zero = sb("zero", [P, 1], F32)
        nc.vector.memset(zero[:], 0.0)
        gs_window = sb("gs_window", [P, T], F32)
        nc.vector.memset(gs_window[:, 0:FILL_SPLIT].bitcast(I32), 0)
        nc.scalar.activation(
            gs_window[:, FILL_SPLIT:T], zero[:].to_broadcast([P, T - FILL_SPLIT]), ACT.Gelu_apprx_tanh
        )
        xs_planes = [sb("xs_plane%d" % o, [P, S], U8) for o in range(2)]
        for o in range(2):
            nc.gpsimd.memset(xs_planes[o][:].bitcast(I32), 0)
        ident = sb("ident", [P, P], F32)
        make_identity(nc, ident[:])

        w1_rows = w1.rearrange("(o p t) c -> o p t c", p=P, t=PACK)
        w1_raw = [sb("w1_raw%d" % o, [P, PACK, H], F32) for o in range(2)]
        x_window = [sb("x_window%d" % o, [P, T], I32) for o in range(2)]

        def load_x(o, a, b):
            nc.sync.dma_start(x_window[o][:, a:b], x_words[o].rearrange("p n t -> p (n t)").bitcast(I32)[:, a:b])

        def move_x_scales(o, rows):
            for r in rows:
                nc.sync.dma_start(
                    xs_planes[o][4 * o + r : P : 32, :].bitcast(I32),
                    xs_gathered[64 * o + 4 * r : 64 * o + 64 : 16, :].bitcast(I32),
                )

        nc.sync.dma_start(w1_raw[0][:], w1_rows[0])
        nc.sync.dma_start(offsets[:], offs)
        nc.sync.dma_start(xs_window[0:P:4, :].bitcast(I32), x_scales.rearrange("o q c -> (o q) c").bitcast(I32))
        nc.sync.dma_start(w2s_raw[0:P:8, :].bitcast(I32), w2_scales[0].bitcast(I32))
        nc.sync.dma_start(w1_raw[1][:], w1_rows[1])
        wsum_cols = sb("wsum_cols", [P, PACK], F32)
        nc.sync.dma_start(wsum_cols[:], wsum.rearrange("(p t) o -> p (t o)", t=PACK))
        for n, (half, table) in enumerate(((0, gain), (0, shift), (1, gain), (1, shift))):
            row, cols = FIRST_ROW + n * ROW_STEP, slice(half * T // 2, (half + 1) * T // 2)
            nc.sync.dma_start(gs_window[row : row + 1, cols], table[0:1, cols])
        load_x(1, 0, X_EARLY)
        load_x(0, 0, T)
        xs_gathered = sb("xs_gathered", [P, S], U8)
        nc.vector.tensor_copy(xs_gathered[:], xs_window[:].indirect(offsets[:]))
        move_x_scales(0, range(4))
        load_x(1, X_EARLY, T)
        move_x_scales(1, range(4))
        w2_raw = sb("w2_raw", [P, 2 * N], U8)
        nc.sync.dma_start(w2_raw[:].bitcast(I32), w2_words[0].bitcast(I32))


        w1_grouped = [sb("w1_grouped%d" % o, [P, H, PACK], BF16) for o in range(2)]
        w1_codes = [sb("w1_codes%d" % o, [P, H], U32) for o in range(2)]
        w1_scales = [sb("w1_scales%d" % o, [P, H], U8) for o in range(2)]
        for o, copy in enumerate((nc.scalar.copy, nc.vector.tensor_copy)):
            copy(
                w1_grouped[o][:].rearrange("p (t m) r -> p m t r", t=PACK),
                w1_raw[o][:].rearrange("p r (m t) -> p m t r", t=PACK),
            )
            nc.vector.quantize_mx(
                w1_codes[o][:].bitcast(FP8X4), w1_scales[o][:], w1_grouped[o][:].rearrange("p c r -> p (c r)")
            )

        wsum_bank = bank(7, "wsum_bank")
        for t in range(PACK):
            nc.tensor.transpose(
                wsum_bank[:, t * P : (t + 1) * P], wsum_cols[:, t : t + 1].to_broadcast([P, P]), ident[:]
            )
        wsum_rows = sb("wsum_rows", [P, H], F32)
        nc.scalar.copy(wsum_rows[:], wsum_bank[:])

        gs_cols = sb("gs_cols", [P, TILES, 2], F32)
        for half in range(2):
            gs_picked = sb("gs_picked%d" % half, [P, S // 2], F32)
            nc.scalar.activation(gs_picked[:], gs_window[:].indirect(offsets[:, 32 * half : 32 * half + 32]), ACT.Copy)
            gs_bank = bank(5 + half, "gs_bank%d" % half)
            for n in range(4):
                nc.tensor.transpose(gs_bank[:, n * P : (n + 1) * P], gs_picked[:, n * P : (n + 1) * P], ident[:])
            gs_parts = sb("gs_parts%d" % half, [P, 4, 4], F32)
            nc.scalar.copy(gs_parts[:], gs_bank[:].rearrange("p (n c) -> p n c", n=4)[:, :, FIRST_ROW:P:ROW_STEP])
            nc.gpsimd.tensor_tensor(gs_cols[:, 4 * half : 4 * half + 4, :], gs_parts[:, :, 0:2], gs_parts[:, :, 2:4], ADD)

        offset_term = {}

        def make_offset_term(j, tag=None):
            offset_term[j] = sb("offset_term%d" % j, [P, PACK, P], F32, tag)
            nc.scalar.activation(
                offset_term[j][:].rearrange("p t m -> p (t m)"), wsum_rows[:], ACT.Copy, scale=gs_cols[:, j, 1:2]
            )

        for j in range(TILES - 1):
            make_offset_term(j)

        y_banks = [bank(j, "y_bank%d" % j) for j in range(TILES)]
        x_picked = {}

        def gather_x(o, first, last, tag=None):
            picked = sb("x_picked%d_%d" % (o, first), [P, (last - first) * P], U32, tag)
            nc.vector.tensor_copy(picked[:], x_window[o][:].bitcast(U32).indirect(offsets[:, 8 * first : 8 * last]))
            for j in range(first, last):
                x_picked[o, j] = picked[:, (j - first) * P : (j - first + 1) * P]

        def first_layer(j, o):
            nc.tensor.matmul_mx(
                y_banks[j][:],
                lhsT=x_picked[o, j].bitcast(FP8X4),
                lhsT_scale=xs_planes[o][4 * o : P, j * P : (j + 1) * P],
                rhs=w1_codes[o][:].bitcast(FP8X4),
                rhs_scale=w1_scales[o][:],
                start=(o == 0),
                stop=(o == 1),
            )

        for first in range(0, TILES, 2):
            gather_x(0, first, first + 2)
            first_layer(first, 0)
            first_layer(first + 1, 0)

        w2s = sb("w2s", [P, PACK, P], U8, "w1_grouped0")
        nc.vector.tensor_copy(w2s[:], w2s_raw[:].rearrange("p (m t) -> p t m", t=PACK))
        w2s_rows = w2s[:].rearrange("p t m -> p (t m)").bitcast(I32)
        for r in range(1, 4):
            nc.sync.dma_start(w2s_rows[r:P:32, :], w2s_rows[8 * r : P : 32, :])

        out_codes = sb("out_codes", [P, S], I32)
        out_scales = sb("out_scales", [P, S], U8)
        out_rows = out_0.rearrange("(p t) j -> p t j", t=PACK)
        out_words = out_1[0].rearrange("p j r -> p (j r)").bitcast(I32)
        units = [(0, 2), (2, 4), (4, 6), (6, 7), (7, 8)]
        word_stores = {2: 0, 4: 2, 6: 4, 8: 6}
        unit_of = {j: u for u, (a, b) in enumerate(units) for j in range(a, b)}
        h_grouped = [sb("h_grouped%d" % u, [P, (b - a) * P, PACK], BF16) for u, (a, b) in enumerate(units)]
        result = [sb("result%d" % n, [P, PACK, 2 * P], F32) for n in range(TILES // 2)]
        out_grouped = [sb("out_grouped%d" % u, [P, (b - a) * P, PACK], BF16) for u, (a, b) in enumerate(units)]
        h_codes, h_scales, out_banks, pre = {}, {}, {}, {}

        def scale(j):
            pre[j] = sb("pre%d" % j, [P, H], F32, {6: "h_grouped0", 7: "h_codes0"}.get(j))
            if j == 0:
                nc.scalar.activation(pre[j][:], y_banks[j][:], ACT.Copy, scale=gs_cols[:, j, 0:1])
            else:
                nc.vector.scalar_tensor_tensor(
                    pre[j][:], y_banks[j][:], gs_cols[:, j, 0:1], offset_term[j][:].rearrange("p t m -> p (t m)"), MULT, ADD
                )

        def hidden(j):
            turned = bank(j, "turned%d" % j)
            for t in range(PACK):
                out = turned[:, t * P : (t + 1) * P]
                nc.tensor.matmul(out, pre[j][:, t * P : (t + 1) * P], ident[:], start=True, stop=j != 0, is_transpose=True)
                if j == 0:
                    nc.tensor.matmul(out, offset_term[j][:, t, :], ident[:], start=False, stop=True, is_transpose=True)
            place = j - units[unit_of[j]][0]
            nc.scalar.activation(
                h_grouped[unit_of[j]][:, place * P : (place + 1) * P, :],
                turned[:].rearrange("p (t j) -> p j t", t=PACK),
                ACT.Gelu_apprx_tanh,
            )

        def quantize_h(u):
            a, b = units[u]
            h_codes[u] = sb("h_codes%d" % u, [P, (b - a) * P], U32)
            h_scales[u] = sb("h_scales%d" % u, [P, (b - a) * P], U8)
            nc.vector.quantize_mx(
                h_codes[u][:].bitcast(FP8X4), h_scales[u][:], h_grouped[u][:].rearrange("p j t -> p (j t)")
            )

        def second_layer(u):
            a, b = units[u]
            width = (b - a) * P
            out_banks[u] = [bank(j, "out_bank%d" % j) for j in range(a, b)]
            for t in range(PACK):
                n, place = divmod(t * width, 512)
                nc.tensor.matmul_mx(
                    out_banks[u][n][:, place : place + width],
                    lhsT=w2_codes[:, t, :].bitcast(U8).bitcast(FP4X4),
                    lhsT_scale=w2s[:, t, :],
                    rhs=h_codes[u][:].bitcast(FP8X4),
                    rhs_scale=h_scales[u][:],
                    start=True,
                    stop=True,
                )

        def leave(u, n, copy):
            a, b = units[u]
            rows = PACK // (b - a)
            part = result[a // 2][:, rows * n : rows * (n + 1), a % 2 * P : (a % 2 + b - a) * P]
            copy(part, out_banks[u][n][:].rearrange("p (t j) -> p t j", t=rows))
            if b % 2 == 0:
                nc.sync.dma_start(
                    out_rows[:, rows * n : rows * (n + 1), (b - 2) * P : b * P],
                    result[a // 2][:, rows * n : rows * (n + 1), :],
                )

        def round_result(u):
            a, b = units[u]
            nc.vector.tensor_copy(
                out_grouped[u][:].rearrange("p (c i) t -> p c t i", i=4),
                result[a // 2][:, :, a % 2 * P : (a % 2 + b - a) * P].rearrange("p t (c i) -> p c t i", i=4),
            )

        def planes(u):
            a, b = units[u]
            cols = slice(a * P, b * P)
            nc.vector.quantize_mx(
                out_codes[:, cols].bitcast(FP8X4), out_scales[:, cols], out_grouped[u][:].rearrange("p j t -> p (j t)")
            )
            if b in word_stores:
                cols = slice(word_stores[b] * P, b * P)
                nc.sync.dma_start(out_words[:, cols], out_codes[:, cols])

        V, A = nc.vector.tensor_copy, nc.scalar.copy
        for first in (0, 2, 4):
            gather_x(1, first, first + 2)
            first_layer(first, 1)
            first_layer(first + 1, 1)
        scale(0)
        w2_codes = sb("w2_codes", [P, PACK, P], U16, "x_picked1_0")
        nc.scalar.copy(w2_codes[:], w2_raw[:].bitcast(U16).rearrange("p (m t) -> p t m", t=PACK))
        make_offset_term(7, "x_picked1_2")
        scale(1)
        scale(2)
        gather_x(1, 6, 8, "offset_term1")
        hidden(0)
        hidden(1)
        hidden(2)
        first_layer(6, 1)
        first_layer(7, 1)
        scale(3)
        hidden(3)
        scale(4)
        hidden(4)
        scale(5)
        hidden(5)
        quantize_h(0)
        second_layer(0)
        scale(6)
        quantize_h(1)
        leave(0, 0, V)
        leave(0, 1, A)
        hidden(6)
        second_layer(1)
        scale(7)
        quantize_h(2)
        leave(1, 0, A)
        leave(1, 1, V)
        hidden(7)
        second_layer(2)
        round_result(0)
        quantize_h(3)
        second_layer(3)
        planes(0)
        quantize_h(4)
        second_layer(4)
        leave(2, 0, A)
        leave(2, 1, A)
        round_result(1)
        leave(3, 0, A)
        round_result(2)
        planes(1)
        leave(4, 0, A)
        nc.scalar.copy(out_grouped[4][:], out_banks[4][0][:].rearrange("p (t j) -> p j t", t=PACK))
        round_result(3)
        planes(2)
        planes(3)
        planes(4)
        for q in range(4):
            engine = nc.sync if q < 2 else nc.scalar
            engine.dma_start(
                out_2[0, 4 * q : 4 * q + 4, :].bitcast(I32), out_scales[32 * q : 32 * q + 4, :].bitcast(I32)
            )
